import numpy as np
import ml_dtypes


def mxq(x, axis, fmt="e4m3"):
    dtype, down = {"e4m3": (ml_dtypes.float8_e4m3fn, 7), "e5m2": (ml_dtypes.float8_e5m2, 14)}[fmt]
    v = np.moveaxis(np.asarray(x, np.float32).astype(ml_dtypes.bfloat16).astype(np.float64), axis, -1)
    blocks = v.reshape(v.shape[:-1] + (-1, 32))
    amax = np.abs(blocks).max(-1, keepdims=True)
    byte = np.maximum(np.where(amax > 0, np.frexp(amax)[1] - 1 + 127, 0) - down, 1)
    scale = np.exp2(byte - 127.0)
    codes = (blocks / scale).astype(np.float32).astype(dtype).astype(np.float64)
    return np.moveaxis((codes * scale).reshape(v.shape), -1, axis)


WIDE = False


def mx_kscale(k):
    if not WIDE:
        return np.ones(k)
    levels = np.array([10, -10, 5, -5, 0])
    if k % 512:
        return np.exp2(np.random.permutation(np.resize(levels, k // 32))).repeat(32)
    a = np.empty((k // 512, 16))
    for p in range(k // 512):
        a[p, :8] = np.random.permutation(np.resize(levels, 8))
        for g in range(8):
            far = levels[np.abs(levels - a[p, g]) >= 10]
            a[p, g + 8] = far[np.random.randint(len(far))]
    return np.exp2(a.ravel()).repeat(32)


def f64(x):
    return np.asarray(x).astype(np.float64)


def striped(idx):
    return np.tile(idx.reshape(-1, 16).T, (8, 1)).astype(np.uint16)


def unstriped(offs):
    return offs[:16].T.reshape(-1).astype(np.int64)


def relu(v):
    return np.maximum(v, 0.0)


K, T, D, S, V, N = 512, 2048, 4, 512, 128, 256


def setup_inputs():
    n = np.random.standard_normal
    s = mx_kscale(K)[:, None]
    return {
        "xT": (n((K, T)) * s).astype(np.float32),
        "w": (n((K, N)) / np.sqrt(K) / s).astype(np.float32),
        "b": (0.3 * n((N, 1))).astype(np.float32),
        "offs": striped(np.random.permutation(T)[:S]),
    }


def reference(xT, w, b, offs):
    idx = unstriped(offs)
    xq = mxq(f64(xT)[:, idx], 0, "e4m3")
    y = mxq(f64(w), 0, "e4m3").T @ xq
    y = relu(y + f64(b))
    return y.reshape(N, V, D).max(axis=2)

@@ -1,0 +1,136 @@
+from contextlib import ExitStack
+
+import concourse.mybir as mybir
+from concourse.masks import make_identity
+
+K, T, D, S, V, N = 512, 2048, 4, 512, 128, 256
+P = 128
+PACK = 4
+FLOPS = 2 * K * S * N
+
+F32 = mybir.dt.float32
+BF16 = mybir.dt.bfloat16
+U32 = mybir.dt.uint32
+U16 = mybir.dt.uint16
+U8 = mybir.dt.uint8
+FP8X4 = mybir.dt.float8_e4m3fn_x4
+RELU = mybir.ActivationFunctionType.Relu
+COPY = mybir.ActivationFunctionType.Copy
+ADD = mybir.AluOpType.add
+MAX = mybir.AluOpType.max
+AXIS_X = mybir.AxisListType.X
+
+HALF = S // 2
+LIST_COLS = S // 16
+
+
+def tile_picked_pool_lin_relu_sub_e_kernel(tc, xT, w, b, offs, out):
+    nc = tc.nc
+    with ExitStack() as ctx:
+        keep = ctx.enter_context(tc.tile_pool(name="keep", bufs=1))
+        psum = ctx.enter_context(tc.psum_pool(name="psum", bufs=1))
+
+        offsets = keep.tile([P, LIST_COLS], U16, name="offsets")
+        planes = [keep.tile([P, T], F32, name=f"plane{t}", align_bytes=64) for t in range(PACK)]
+        w_raw = keep.tile([P, PACK, N], F32, name="w_raw", align_bytes=64)
+        identity = keep.tile([P, P], F32, name="identity")
+        bias_rows = keep.tile([P, P], F32, name="bias_rows")
+        bias_turned = psum.tile([P, P], F32, name="bias_turned")
+        bias = keep.tile([P, 2], F32, name="bias")
+        x_grouped = [keep.tile([P, HALF, PACK], BF16, name=f"x_grouped{h}", align_bytes=64) for h in range(2)]
+        x_codes = keep.tile([P, S], U32, name="x_codes", align_bytes=64)
+        x_scales = keep.tile([P, S], U8, name="x_scales", align_bytes=64)
+        w_grouped = [keep.tile([P, P, PACK], BF16, name=f"w_grouped{h}", align_bytes=64) for h in range(2)]
+        w_codes = keep.tile([P, N], U32, name="w_codes", align_bytes=64)
+        w_scales = keep.tile([P, N], U8, name="w_scales", align_bytes=64)
+        accs = [[psum.tile([P, HALF], F32, name=f"acc{m}{h}") for h in range(2)] for m in range(2)]
+        pooled = [keep.tile([P, V], F32, name=f"pooled{h}") for h in range(2)]
+        result = [keep.tile([P, V], F32, name=f"result{h}") for h in range(2)]
+
+        x_rows = xT.rearrange("(p j) t -> p j t", j=PACK)
+        lcols = [slice(h * LIST_COLS // 2, (h + 1) * LIST_COLS // 2) for h in range(2)]
+        cols = [slice(h * HALF, (h + 1) * HALF) for h in range(2)]
+        vcols = [slice(h * V // 2, (h + 1) * V // 2) for h in range(2)]
+        mcols = [slice(h * P, (h + 1) * P) for h in range(2)]
+        chunks = [[0,2048]]
+        w_rows = w.rearrange("(p j) m -> p j m", j=PACK)
+        nc.sync.dma_start(planes[0][:], x_rows[:, 0, :])
+        nc.sync.dma_start(offsets[:], offs)
+        nc.gpsimd.memset(bias_rows[:], 0.0)
+        for t in (2, 3):
+            nc.sync.dma_start(planes[t][:], x_rows[:, t, :])
+        for a, z in chunks:
+            nc.sync.dma_start(planes[1][:, a:z], x_rows[:, 1, a:z])
+        nc.sync.dma_start(w_raw[:], w_rows)
+        nc.sync.dma_start(bias_rows[0:2, :], b.rearrange("(h p) o -> h (p o)", p=P))
+
+        make_identity(nc, identity[:])
+
+        def gather(h, t):
+            nc.vector.tensor_copy(x_grouped[h][:, :, t], planes[t][:].indirect(offsets[:, lcols[h]]))
+
+        def quantize_x(h):
+            nc.vector.quantize_mx(
+                out=x_codes[:, cols[h]].bitcast(FP8X4),
+                scales=x_scales[:, cols[h]],
+                in_=x_grouped[h][:].rearrange("p n j -> p (n j)"),
+            )
+
+        def quantize_w(h):
+            nc.vector.quantize_mx(
+                out=w_codes[:, mcols[h]].bitcast(FP8X4),
+                scales=w_scales[:, mcols[h]],
+                in_=w_grouped[h][:].rearrange("p n j -> p (n j)"),
+            )
+
+        def product(m, h):
+            nc.tensor.matmul_mx(
+                out=accs[m][h][:],
+                lhsT=w_codes[:, mcols[m]].bitcast(FP8X4),
+                lhsT_scale=w_scales[:, mcols[m]],
+                rhs=x_codes[:, cols[h]].bitcast(FP8X4),
+                rhs_scale=x_scales[:, cols[h]],
+                start=True,
+                stop=True,
+            )
+
+        def grouped_sums(m, h):
+            return accs[m][h][:].rearrange("p (v d) -> p v d", d=D)
+
+        def w_copy_s(m):
+            nc.scalar.copy(
+                w_grouped[m][:].rearrange("p (c i) j -> p c j i", i=4),
+                w_raw[:, :, mcols[m]].rearrange("p j (c i) -> p c j i", i=4),
+            )
+
+        def largest(m, h):
+            nc.vector.tensor_reduce(out=pooled[m][:, vcols[h]], in_=grouped_sums(m, h), axis=AXIS_X, op=MAX)
+
+        def finish(m, h):
+            nc.scalar.activation(result[m][:, vcols[h]], pooled[m][:, vcols[h]], RELU, bias=bias[:, m : m + 1])
+
+        def store(m):
+            nc.sync.dma_start(out[m * P : (m + 1) * P, :], result[m][:])
+
+        gather(0, 0)
+        gather(1, 0)
+        for t in (2, 3, 1):
+            gather(0, t)
+            gather(1, t)
+        w_copy_s(0)
+        w_copy_s(1)
+        quantize_x(0)
+        quantize_w(0)
+        product(0, 0)
+        quantize_x(1)
+        product(0, 1)
+        quantize_w(1)
+        nc.tensor.transpose(bias_turned[:], bias_rows[:], identity[:])
+        nc.scalar.copy(bias[:], bias_turned[:, 0:2])
+        product(1, 0)
+        product(1, 1)
+        for m in range(2):
+            for h in range(2):
+                largest(m, h)
+                finish(m, h)
+            store(m)

@@ -1,7 +1,6 @@
 from contextlib import ExitStack
 
 import concourse.mybir as mybir
-from concourse.masks import make_identity
 
 K, T, D, S, V, N = 512, 2048, 4, 512, 128, 256
 P = 128
@@ -33,10 +32,8 @@ def tile_picked_pool_lin_relu_sub_e_kernel(tc, xT, w, b, offs, out):
         offsets = keep.tile([P, LIST_COLS], U16, name="offsets")
         planes = [keep.tile([P, T], F32, name=f"plane{t}", align_bytes=64) for t in range(PACK)]
         w_raw = keep.tile([P, PACK, N], F32, name="w_raw", align_bytes=64)
-        identity = keep.tile([P, P], F32, name="identity")
-        bias_rows = keep.tile([P, P], F32, name="bias_rows")
-        bias_turned = psum.tile([P, P], F32, name="bias_turned")
-        bias = keep.tile([P, 2], F32, name="bias")
+        bias_rows = keep.tile([P, P], F32, name="bias_rows", align_bytes=64)
+        bias = keep.tile([P, P], F32, name="bias", align_bytes=64)
         x_grouped = [keep.tile([P, HALF, PACK], BF16, name=f"x_grouped{h}", align_bytes=64) for h in range(2)]
         x_codes = keep.tile([P, S], U32, name="x_codes", align_bytes=64)
         x_scales = keep.tile([P, S], U8, name="x_scales", align_bytes=64)
@@ -52,19 +49,18 @@ def tile_picked_pool_lin_relu_sub_e_kernel(tc, xT, w, b, offs, out):
         cols = [slice(h * HALF, (h + 1) * HALF) for h in range(2)]
         vcols = [slice(h * V // 2, (h + 1) * V // 2) for h in range(2)]
         mcols = [slice(h * P, (h + 1) * P) for h in range(2)]
-        chunks = [[0,2048]]
         w_rows = w.rearrange("(p j) m -> p j m", j=PACK)
         nc.sync.dma_start(planes[0][:], x_rows[:, 0, :])
         nc.sync.dma_start(offsets[:], offs)
-        nc.gpsimd.memset(bias_rows[:], 0.0)
-        for t in (2, 3):
+        nc.vector.memset(bias_rows[:], 0.0)
+        nc.sync.dma_start(planes[2][:], x_rows[:, 2, :])
+        nc.sync.dma_start(
+            bias_rows[0:P:32, 0:64].rearrange("q (h i) -> q h i", h=2),
+            b.rearrange("(h q i) o -> q h (i o)", h=2, i=32),
+        )
+        for t in (3, 1):
             nc.sync.dma_start(planes[t][:], x_rows[:, t, :])
-        for a, z in chunks:
-            nc.sync.dma_start(planes[1][:, a:z], x_rows[:, 1, a:z])
         nc.sync.dma_start(w_raw[:], w_rows)
-        nc.sync.dma_start(bias_rows[0:2, :], b.rearrange("(h p) o -> h (p o)", p=P))
-
-        make_identity(nc, identity[:])
 
         def gather(h, t):
             nc.vector.tensor_copy(x_grouped[h][:, :, t], planes[t][:].indirect(offsets[:, lcols[h]]))
@@ -107,13 +103,14 @@ def tile_picked_pool_lin_relu_sub_e_kernel(tc, xT, w, b, offs, out):
             nc.vector.tensor_reduce(out=pooled[m][:, vcols[h]], in_=grouped_sums(m, h), axis=AXIS_X, op=MAX)
 
         def finish(m, h):
-            nc.scalar.activation(result[m][:, vcols[h]], pooled[m][:, vcols[h]], RELU, bias=bias[:, m : m + 1])
+            nc.scalar.activation(result[m][:, vcols[h]], pooled[m][:, vcols[h]], RELU, bias=bias[:, 32 * m : 32 * m + 1])
 
         def store(m):
             nc.sync.dma_start(out[m * P : (m + 1) * P, :], result[m][:])
 
         gather(0, 0)
         gather(1, 0)
+        nc.vector.transpose(bias[:], bias_rows[:])
         for t in (2, 3, 1):
             gather(0, t)
             gather(1, t)
@@ -125,8 +122,6 @@ def tile_picked_pool_lin_relu_sub_e_kernel(tc, xT, w, b, offs, out):
         quantize_x(1)
         product(0, 1)
         quantize_w(1)
-        nc.tensor.transpose(bias_turned[:], bias_rows[:], identity[:])
-        nc.scalar.copy(bias[:], bias_turned[:, 0:2])
         product(1, 0)
         product(1, 1)
         for m in range(2):

@@ -30,7 +30,9 @@ def tile_picked_pool_lin_relu_sub_e_kernel(tc, xT, w, b, offs, out):
         psum = ctx.enter_context(tc.psum_pool(name="psum", bufs=1))
 
         offsets = keep.tile([P, LIST_COLS], U16, name="offsets")
-        planes = [keep.tile([P, T], F32, name=f"plane{t}", align_bytes=64) for t in range(PACK)]
+        first_pair = keep.tile([P, 2, T], F32, name="first_pair", align_bytes=64)
+        planes = {t: keep.tile([P, T], F32, name=f"plane{t}", align_bytes=64) for t in (2, 3)}
+        picked_pair = [keep.tile([P, 2, HALF], F32, name=f"picked_pair{h}", align_bytes=64) for h in range(2)]
         w_raw = keep.tile([P, PACK, N], F32, name="w_raw", align_bytes=64)
         bias_rows = keep.tile([P, P], F32, name="bias_rows", align_bytes=64)
         bias = keep.tile([P, P], F32, name="bias", align_bytes=64)
@@ -50,7 +52,7 @@ def tile_picked_pool_lin_relu_sub_e_kernel(tc, xT, w, b, offs, out):
         vcols = [slice(h * V // 2, (h + 1) * V // 2) for h in range(2)]
         mcols = [slice(h * P, (h + 1) * P) for h in range(2)]
         w_rows = w.rearrange("(p j) m -> p j m", j=PACK)
-        nc.sync.dma_start(planes[0][:], x_rows[:, 0, :])
+        nc.sync.dma_start(first_pair[:], x_rows[:, 0:2, :])
         nc.sync.dma_start(offsets[:], offs)
         nc.vector.memset(bias_rows[:], 0.0)
         nc.sync.dma_start(planes[2][:], x_rows[:, 2, :])
@@ -58,12 +60,17 @@ def tile_picked_pool_lin_relu_sub_e_kernel(tc, xT, w, b, offs, out):
             bias_rows[0:P:32, 0:64].rearrange("q (h i) -> q h i", h=2),
             b.rearrange("(h q i) o -> q h (i o)", h=2, i=32),
         )
-        for t in (3, 1):
-            nc.sync.dma_start(planes[t][:], x_rows[:, t, :])
+        nc.sync.dma_start(planes[3][:], x_rows[:, 3, :])
         nc.sync.dma_start(w_raw[:], w_rows)
 
         def gather(h, t):
             nc.vector.tensor_copy(x_grouped[h][:, :, t], planes[t][:].indirect(offsets[:, lcols[h]]))
+
+        def gather_plain(h, t):
+            nc.vector.tensor_copy(picked_pair[h][:, t, :], first_pair[:, t, :].indirect(offsets[:, lcols[h]]))
+
+        def weave_pair(h):
+            nc.scalar.copy(x_grouped[h][:, :, 0:2], picked_pair[h][:].rearrange("p j n -> p n j"))
 
         def quantize_x(h):
             nc.vector.quantize_mx(
@@ -108,12 +115,15 @@ def tile_picked_pool_lin_relu_sub_e_kernel(tc, xT, w, b, offs, out):
         def store(m):
             nc.sync.dma_start(out[m * P : (m + 1) * P, :], result[m][:])
 
-        gather(0, 0)
-        gather(1, 0)
+        for h in range(2):
+            gather_plain(h, 0)
+            gather_plain(h, 1)
+        for h in range(2):
+            gather(h, 2)
+            weave_pair(h)
         nc.vector.transpose(bias[:], bias_rows[:])
-        for t in (2, 3, 1):
-            gather(0, t)
-            gather(1, t)
+        for h in range(2):
+            gather(h, 3)
         w_copy_s(0)
         w_copy_s(1)
         quantize_x(0)

@@ -14,12 +14,13 @@ U16 = mybir.dt.uint16
 U8 = mybir.dt.uint8
 FP8X4 = mybir.dt.float8_e4m3fn_x4
 RELU = mybir.ActivationFunctionType.Relu
-COPY = mybir.ActivationFunctionType.Copy
+IDENTITY = mybir.ActivationFunctionType.Identity
 ADD = mybir.AluOpType.add
 MAX = mybir.AluOpType.max
 AXIS_X = mybir.AxisListType.X
 
 HALF = S // 2
+QUARTER = S // 4
 LIST_COLS = S // 16
 
 
@@ -34,22 +35,23 @@ def tile_picked_pool_lin_relu_sub_e_kernel(tc, xT, w, b, offs, out):
         planes = {t: keep.tile([P, T], F32, name=f"plane{t}", align_bytes=64) for t in (2, 3)}
         picked_pair = [keep.tile([P, 2, HALF], F32, name=f"picked_pair{h}", align_bytes=64) for h in range(2)]
         w_raw = keep.tile([P, PACK, N], F32, name="w_raw", align_bytes=64)
-        bias_rows = keep.tile([P, P], F32, name="bias_rows", align_bytes=64)
+        bias_rows = keep.tile([P, P], F32, name="bias_rows", tag="rows_then_scales", align_bytes=64)
         bias = keep.tile([P, P], F32, name="bias", align_bytes=64)
         x_grouped = [keep.tile([P, HALF, PACK], BF16, name=f"x_grouped{h}", align_bytes=64) for h in range(2)]
         x_codes = keep.tile([P, S], U32, name="x_codes", align_bytes=64)
-        x_scales = keep.tile([P, S], U8, name="x_scales", align_bytes=64)
+        x_scales = [keep.tile([P, HALF], U8, name="x_scales0", align_bytes=64)]
         w_grouped = [keep.tile([P, P, PACK], BF16, name=f"w_grouped{h}", align_bytes=64) for h in range(2)]
         w_codes = keep.tile([P, N], U32, name="w_codes", align_bytes=64)
         w_scales = keep.tile([P, N], U8, name="w_scales", align_bytes=64)
-        accs = [[psum.tile([P, HALF], F32, name=f"acc{m}{h}") for h in range(2)] for m in range(2)]
+        pieces = [(0, 0, HALF), (0, HALF, HALF), (1, 0, HALF), (1, HALF, QUARTER), (1, HALF + QUARTER, QUARTER)]
+        accs = {(m, a): psum.tile([P, n], F32, name=f"acc{m}_{a}") for m, a, n in pieces}
+        staged = keep.tile([P, QUARTER], F32, name="staged")
         pooled = [keep.tile([P, V], F32, name=f"pooled{h}") for h in range(2)]
         result = [keep.tile([P, V], F32, name=f"result{h}") for h in range(2)]
 
         x_rows = xT.rearrange("(p j) t -> p j t", j=PACK)
         lcols = [slice(h * LIST_COLS // 2, (h + 1) * LIST_COLS // 2) for h in range(2)]
         cols = [slice(h * HALF, (h + 1) * HALF) for h in range(2)]
-        vcols = [slice(h * V // 2, (h + 1) * V // 2) for h in range(2)]
         mcols = [slice(h * P, (h + 1) * P) for h in range(2)]
         w_rows = w.rearrange("(p j) m -> p j m", j=PACK)
         nc.sync.dma_start(first_pair[:], x_rows[:, 0:2, :])
@@ -75,7 +77,7 @@ def tile_picked_pool_lin_relu_sub_e_kernel(tc, xT, w, b, offs, out):
         def quantize_x(h):
             nc.vector.quantize_mx(
                 out=x_codes[:, cols[h]].bitcast(FP8X4),
-                scales=x_scales[:, cols[h]],
+                scales=x_scales[h][:],
                 in_=x_grouped[h][:].rearrange("p n j -> p (n j)"),
             )
 
@@ -86,19 +88,16 @@ def tile_picked_pool_lin_relu_sub_e_kernel(tc, xT, w, b, offs, out):
                 in_=w_grouped[h][:].rearrange("p n j -> p (n j)"),
             )
 
-        def product(m, h):
+        def product(m, a, n):
             nc.tensor.matmul_mx(
-                out=accs[m][h][:],
+                out=accs[m, a][:],
                 lhsT=w_codes[:, mcols[m]].bitcast(FP8X4),
                 lhsT_scale=w_scales[:, mcols[m]],
-                rhs=x_codes[:, cols[h]].bitcast(FP8X4),
-                rhs_scale=x_scales[:, cols[h]],
+                rhs=x_codes[:, a : a + n].bitcast(FP8X4),
+                rhs_scale=x_scales[a // HALF][:, a % HALF : a % HALF + n],
                 start=True,
                 stop=True,
             )
-
-        def grouped_sums(m, h):
-            return accs[m][h][:].rearrange("p (v d) -> p v d", d=D)
 
         def w_copy_s(m):
             nc.scalar.copy(
@@ -106,11 +105,16 @@ def tile_picked_pool_lin_relu_sub_e_kernel(tc, xT, w, b, offs, out):
                 w_raw[:, :, mcols[m]].rearrange("p j (c i) -> p c j i", i=4),
             )
 
-        def largest(m, h):
-            nc.vector.tensor_reduce(out=pooled[m][:, vcols[h]], in_=grouped_sums(m, h), axis=AXIS_X, op=MAX)
+        def largest(dst, src):
+            nc.vector.tensor_reduce(out=dst, in_=src.rearrange("p (v d) -> p v d", d=D), axis=AXIS_X, op=MAX)
 
-        def finish(m, h):
-            nc.scalar.activation(result[m][:, vcols[h]], pooled[m][:, vcols[h]], RELU, bias=bias[:, 32 * m : 32 * m + 1])
+        def bias_relu(m, dst, src):
+            nc.scalar.activation(dst, src, RELU, bias=bias[:, 32 * m : 32 * m + 1])
+
+        def pool_then_finish(m, a, n):
+            v = slice(a // D, (a + n) // D)
+            largest(pooled[m][:, v], accs[m, a][:])
+            bias_relu(m, result[m][:, v], pooled[m][:, v])
 
         def store(m):
             nc.sync.dma_start(out[m * P : (m + 1) * P, :], result[m][:])
@@ -124,18 +128,28 @@ def tile_picked_pool_lin_relu_sub_e_kernel(tc, xT, w, b, offs, out):
         nc.vector.transpose(bias[:], bias_rows[:])
         for h in range(2):
             gather(h, 3)
-        w_copy_s(0)
+        nc.scalar.activation(
+            w_grouped[0][:].rearrange("p (c i) j -> p c j i", i=4),
+            w_raw[:, :, mcols[0]].rearrange("p j (c i) -> p c j i", i=4),
+            IDENTITY,
+            bias=bias_rows[:, P - 1 : P],
+        )
         w_copy_s(1)
+        x_scales.append(keep.tile([P, HALF], U8, name="x_scales1", tag="rows_then_scales", align_bytes=64))
         quantize_x(0)
         quantize_w(0)
-        product(0, 0)
+        product(*pieces[0])
         quantize_x(1)
-        product(0, 1)
+        product(*pieces[1])
         quantize_w(1)
-        product(1, 0)
-        product(1, 1)
-        for m in range(2):
-            for h in range(2):
-                largest(m, h)
-                finish(m, h)
-            store(m)
+        for piece in pieces[2:]:
+            product(*piece)
+        pool_then_finish(*pieces[0])
+        pool_then_finish(*pieces[1])
+        store(0)
+        m, a, n = pieces[3]
+        bias_relu(m, staged[:], accs[m, a][:])
+        pool_then_finish(*pieces[2])
+        pool_then_finish(*pieces[4])
+        largest(result[m][:, a // D : (a + n) // D], staged[:])
+        store(1)

@@ -122,9 +122,10 @@ def tile_picked_pool_lin_relu_sub_e_kernel(tc, xT, w, b, offs, out):
         for h in range(2):
             gather_plain(h, 0)
             gather_plain(h, 1)
-        for h in range(2):
-            gather(h, 2)
-            weave_pair(h)
+        weave_pair(0)
+        gather(1, 2)
+        weave_pair(1)
+        gather(0, 2)
         nc.vector.transpose(bias[:], bias_rows[:])
         for h in range(2):
             gather(h, 3)

@@ -58,7 +58,7 @@ def tile_picked_pool_lin_relu_sub_e_kernel(tc, xT, w, b, offs, out):
         nc.sync.dma_start(offsets[:], offs)
         nc.vector.memset(bias_rows[:], 0.0)
         nc.sync.dma_start(planes[2][:], x_rows[:, 2, :])
-        nc.sync.dma_start(
+        nc.scalar.dma_start(
             bias_rows[0:P:32, 0:64].rearrange("q (h i) -> q h i", h=2),
             b.rearrange("(h q i) o -> q h (i o)", h=2, i=32),
         )

@@ -35,8 +35,8 @@ def tile_picked_pool_lin_relu_sub_e_kernel(tc, xT, w, b, offs, out):
         planes = {t: keep.tile([P, T], F32, name=f"plane{t}", align_bytes=64) for t in (2, 3)}
         picked_pair = [keep.tile([P, 2, HALF], F32, name=f"picked_pair{h}", align_bytes=64) for h in range(2)]
         w_raw = keep.tile([P, PACK, N], F32, name="w_raw", align_bytes=64)
-        bias_rows = keep.tile([P, P], F32, name="bias_rows", tag="rows_then_scales", align_bytes=64)
-        bias = keep.tile([P, P], F32, name="bias", align_bytes=64)
+        zeros = keep.tile([P, 64], F32, name="zeros", tag="rows_then_scales", align_bytes=64)
+        bias = keep.tile([P, 2, 8], F32, name="bias", align_bytes=64)
         x_grouped = [keep.tile([P, HALF, PACK], BF16, name=f"x_grouped{h}", align_bytes=64) for h in range(2)]
         x_codes = keep.tile([P, S], U32, name="x_codes", align_bytes=64)
         x_scales = [keep.tile([P, HALF], U8, name="x_scales0", align_bytes=64)]
@@ -56,14 +56,12 @@ def tile_picked_pool_lin_relu_sub_e_kernel(tc, xT, w, b, offs, out):
         w_rows = w.rearrange("(p j) m -> p j m", j=PACK)
         nc.sync.dma_start(first_pair[:], x_rows[:, 0:2, :])
         nc.sync.dma_start(offsets[:], offs)
-        nc.vector.memset(bias_rows[:], 0.0)
+        nc.vector.memset(zeros[:, 0:1], 0.0)
         nc.sync.dma_start(planes[2][:], x_rows[:, 2, :])
-        nc.scalar.dma_start(
-            bias_rows[0:P:32, 0:64].rearrange("q (h i) -> q h i", h=2),
-            b.rearrange("(h q i) o -> q h (i o)", h=2, i=32),
-        )
         nc.sync.dma_start(planes[3][:], x_rows[:, 3, :])
         nc.sync.dma_start(w_raw[:], w_rows)
+        with nc.allow_non_contiguous_dma(reason="one bias value a partition and channel tile"):
+            nc.sync.dma_start(bias[:, :, 0:1], b.rearrange("(h p) o -> p h o", h=2))
 
         def gather(h, t):
             nc.vector.tensor_copy(x_grouped[h][:, :, t], planes[t][:].indirect(offsets[:, lcols[h]]))
@@ -109,7 +107,7 @@ def tile_picked_pool_lin_relu_sub_e_kernel(tc, xT, w, b, offs, out):
             nc.vector.tensor_reduce(out=dst, in_=src.rearrange("p (v d) -> p v d", d=D), axis=AXIS_X, op=MAX)
 
         def bias_relu(m, dst, src):
-            nc.scalar.activation(dst, src, RELU, bias=bias[:, 32 * m : 32 * m + 1])
+            nc.scalar.activation(dst, src, RELU, bias=bias[:, m, 0:1])
 
         def pool_then_finish(m, a, n):
             v = slice(a // D, (a + n) // D)
@@ -126,14 +124,13 @@ def tile_picked_pool_lin_relu_sub_e_kernel(tc, xT, w, b, offs, out):
         gather(1, 2)
         weave_pair(1)
         gather(0, 2)
-        nc.vector.transpose(bias[:], bias_rows[:])
         for h in range(2):
             gather(h, 3)
         nc.scalar.activation(
             w_grouped[0][:].rearrange("p (c i) j -> p c j i", i=4),
             w_raw[:, :, mcols[0]].rearrange("p j (c i) -> p c j i", i=4),
             IDENTITY,
-            bias=bias_rows[:, P - 1 : P],
+            bias=zeros[:, 0:1],
         )
         w_copy_s(1)
         x_scales.append(keep.tile([P, HALF], U8, name="x_scales1", tag="rows_then_scales", align_bytes=64))

@@ -47,7 +47,8 @@ def tile_picked_pool_lin_relu_sub_e_kernel(tc, xT, w, b, offs, out):
         accs = {(m, a): psum.tile([P, n], F32, name=f"acc{m}_{a}") for m, a, n in pieces}
         staged = keep.tile([P, QUARTER], F32, name="staged")
         pooled = [keep.tile([P, V], F32, name=f"pooled{h}") for h in range(2)]
-        result = [keep.tile([P, V], F32, name=f"result{h}") for h in range(2)]
+        results = keep.tile([P, 2, V], F32, name="results")
+        result = [results[:, h, :] for h in range(2)]
 
         x_rows = xT.rearrange("(p j) t -> p j t", j=PACK)
         lcols = [slice(h * LIST_COLS // 2, (h + 1) * LIST_COLS // 2) for h in range(2)]
@@ -114,8 +115,6 @@ def tile_picked_pool_lin_relu_sub_e_kernel(tc, xT, w, b, offs, out):
             largest(pooled[m][:, v], accs[m, a][:])
             bias_relu(m, result[m][:, v], pooled[m][:, v])
 
-        def store(m):
-            nc.sync.dma_start(out[m * P : (m + 1) * P, :], result[m][:])
 
         for h in range(2):
             gather_plain(h, 0)
@@ -144,10 +143,9 @@ def tile_picked_pool_lin_relu_sub_e_kernel(tc, xT, w, b, offs, out):
             product(*piece)
         pool_then_finish(*pieces[0])
         pool_then_finish(*pieces[1])
-        store(0)
         m, a, n = pieces[3]
         bias_relu(m, staged[:], accs[m, a][:])
         pool_then_finish(*pieces[2])
         pool_then_finish(*pieces[4])
         largest(result[m][:, a // D : (a + n) // D], staged[:])
-        store(1)
+        nc.sync.dma_start(out.rearrange("(m p) v -> p m v", m=2), results[:])

@@ -36,14 +36,14 @@ def tile_picked_pool_lin_relu_sub_e_kernel(tc, xT, w, b, offs, out):
         picked_pair = [keep.tile([P, 2, HALF], F32, name=f"picked_pair{h}", align_bytes=64) for h in range(2)]
         w_raw = keep.tile([P, PACK, N], F32, name="w_raw", align_bytes=64)
         zeros = keep.tile([P, 64], F32, name="zeros", tag="rows_then_scales", align_bytes=64)
-        bias = keep.tile([P, 2, 8], F32, name="bias", align_bytes=64)
+        bias = keep.tile([P, 2], F32, name="bias", align_bytes=64)
         x_grouped = [keep.tile([P, HALF, PACK], BF16, name=f"x_grouped{h}", align_bytes=64) for h in range(2)]
         x_codes = keep.tile([P, S], U32, name="x_codes", align_bytes=64)
         x_scales = [keep.tile([P, HALF], U8, name="x_scales0", align_bytes=64)]
         w_grouped = [keep.tile([P, P, PACK], BF16, name=f"w_grouped{h}", align_bytes=64) for h in range(2)]
         w_codes = keep.tile([P, N], U32, name="w_codes", align_bytes=64)
         w_scales = keep.tile([P, N], U8, name="w_scales", align_bytes=64)
-        pieces = [(0, 0, HALF), (0, HALF, HALF), (1, 0, HALF), (1, HALF, QUARTER), (1, HALF + QUARTER, QUARTER)]
+        pieces = [(0, 0, QUARTER), (0, QUARTER, QUARTER), (0, HALF, HALF)] + [(1, q * QUARTER, QUARTER) for q in range(4)]
         accs = {(m, a): psum.tile([P, n], F32, name=f"acc{m}_{a}") for m, a, n in pieces}
         staged = keep.tile([P, QUARTER], F32, name="staged")
         pooled = [keep.tile([P, V], F32, name=f"pooled{h}") for h in range(2)]
@@ -61,8 +61,7 @@ def tile_picked_pool_lin_relu_sub_e_kernel(tc, xT, w, b, offs, out):
         nc.sync.dma_start(planes[2][:], x_rows[:, 2, :])
         nc.sync.dma_start(planes[3][:], x_rows[:, 3, :])
         nc.sync.dma_start(w_raw[:], w_rows)
-        with nc.allow_non_contiguous_dma(reason="one bias value a partition and channel tile"):
-            nc.sync.dma_start(bias[:, :, 0:1], b.rearrange("(h p) o -> p h o", h=2))
+        nc.sync.dma_start(bias[:], b.rearrange("(p h) o -> p (h o)", h=2))
 
         def gather(h, t):
             nc.vector.tensor_copy(x_grouped[h][:, :, t], planes[t][:].indirect(offsets[:, lcols[h]]))
@@ -101,20 +100,26 @@ def tile_picked_pool_lin_relu_sub_e_kernel(tc, xT, w, b, offs, out):
         def w_copy_s(m):
             nc.scalar.copy(
                 w_grouped[m][:].rearrange("p (c i) j -> p c j i", i=4),
-                w_raw[:, :, mcols[m]].rearrange("p j (c i) -> p c j i", i=4),
+                w_raw[:].rearrange("p j (c i h) -> p h c j i", i=4, h=2)[:, m],
             )
 
         def largest(dst, src):
             nc.vector.tensor_reduce(out=dst, in_=src.rearrange("p (v d) -> p v d", d=D), axis=AXIS_X, op=MAX)
 
         def bias_relu(m, dst, src):
-            nc.scalar.activation(dst, src, RELU, bias=bias[:, m, 0:1])
+            nc.scalar.activation(dst, src, RELU, bias=bias[:, m : m + 1])
 
         def pool_then_finish(m, a, n):
             v = slice(a // D, (a + n) // D)
             largest(pooled[m][:, v], accs[m, a][:])
             bias_relu(m, result[m][:, v], pooled[m][:, v])
 
+
+        def store(a, z):
+            nc.sync.dma_start(
+                out.rearrange("(p m) v -> p (m v)", m=2)[:, a:z],
+                results[:].rearrange("p m v -> p (m v)")[:, a:z],
+            )
 
         for h in range(2):
             gather_plain(h, 0)
@@ -127,7 +132,7 @@ def tile_picked_pool_lin_relu_sub_e_kernel(tc, xT, w, b, offs, out):
             gather(h, 3)
         nc.scalar.activation(
             w_grouped[0][:].rearrange("p (c i) j -> p c j i", i=4),
-            w_raw[:, :, mcols[0]].rearrange("p j (c i) -> p c j i", i=4),
+            w_raw[:].rearrange("p j (c i h) -> p h c j i", i=4, h=2)[:, 0],
             IDENTITY,
             bias=zeros[:, 0:1],
         )
@@ -136,16 +141,19 @@ def tile_picked_pool_lin_relu_sub_e_kernel(tc, xT, w, b, offs, out):
         quantize_x(0)
         quantize_w(0)
         product(*pieces[0])
-        quantize_x(1)
         product(*pieces[1])
+        quantize_x(1)
+        product(*pieces[2])
         quantize_w(1)
-        for piece in pieces[2:]:
+        for piece in pieces[3:]:
             product(*piece)
-        pool_then_finish(*pieces[0])
-        pool_then_finish(*pieces[1])
-        m, a, n = pieces[3]
+        for piece in pieces[:3]:
+            pool_then_finish(*piece)
+        m, a, n = pieces[5]
         bias_relu(m, staged[:], accs[m, a][:])
-        pool_then_finish(*pieces[2])
+        pool_then_finish(*pieces[3])
         pool_then_finish(*pieces[4])
+        store(0, 3 * V // 2)
+        pool_then_finish(*pieces[6])
         largest(result[m][:, a // D : (a + n) // D], staged[:])
-        nc.sync.dma_start(out.rearrange("(m p) v -> p m v", m=2), results[:])
+        store(3 * V // 2, 2 * V)

@@ -43,9 +43,8 @@ def tile_picked_pool_lin_relu_sub_e_kernel(tc, xT, w, b, offs, out):
         w_grouped = [keep.tile([P, P, PACK], BF16, name=f"w_grouped{h}", align_bytes=64) for h in range(2)]
         w_codes = keep.tile([P, N], U32, name="w_codes", align_bytes=64)
         w_scales = keep.tile([P, N], U8, name="w_scales", align_bytes=64)
-        pieces = [(0, 0, QUARTER), (0, QUARTER, QUARTER), (0, HALF, HALF)] + [(1, q * QUARTER, QUARTER) for q in range(4)]
+        pieces = [(m, q * QUARTER, QUARTER) for m in range(2) for q in range(4)]
         accs = {(m, a): psum.tile([P, n], F32, name=f"acc{m}_{a}") for m, a, n in pieces}
-        staged = keep.tile([P, QUARTER], F32, name="staged")
         pooled = [keep.tile([P, V], F32, name=f"pooled{h}") for h in range(2)]
         results = keep.tile([P, 2, V], F32, name="results")
         result = [results[:, h, :] for h in range(2)]
@@ -144,16 +143,21 @@ def tile_picked_pool_lin_relu_sub_e_kernel(tc, xT, w, b, offs, out):
         product(*pieces[1])
         quantize_x(1)
         product(*pieces[2])
+        product(*pieces[3])
         quantize_w(1)
-        for piece in pieces[3:]:
+        for piece in pieces[4:]:
             product(*piece)
-        for piece in pieces[:3]:
-            pool_then_finish(*piece)
-        m, a, n = pieces[5]
-        bias_relu(m, staged[:], accs[m, a][:])
-        pool_then_finish(*pieces[3])
-        pool_then_finish(*pieces[4])
+        for m, a, n in pieces[:4]:
+            largest(pooled[m][:, a // D : (a + n) // D], accs[m, a][:])
+        bias_relu(0, result[0][:], pooled[0][:])
+        for m, a, n in pieces[4:6]:
+            largest(pooled[m][:, a // D : (a + n) // D], accs[m, a][:])
+        bias_relu(1, result[1][:, : V // 2], pooled[1][:, : V // 2])
         store(0, 3 * V // 2)
-        pool_then_finish(*pieces[6])
-        largest(result[m][:, a // D : (a + n) // D], staged[:])
+        for m, a, n in pieces[6:]:
+            largest(pooled[m][:, a // D : (a + n) // D], accs[m, a][:])
+        nc.vector.tensor_scalar(
+            out=result[1][:, V // 2 :], in0=pooled[1][:, V // 2 :],
+            scalar1=bias[:, 1:2], scalar2=0.0, op0=ADD, op1=MAX,
+        )
         store(3 * V // 2, 2 * V)

@@ -150,14 +150,14 @@ def tile_picked_pool_lin_relu_sub_e_kernel(tc, xT, w, b, offs, out):
         for m, a, n in pieces[:4]:
             largest(pooled[m][:, a // D : (a + n) // D], accs[m, a][:])
         bias_relu(0, result[0][:], pooled[0][:])
-        for m, a, n in pieces[4:6]:
+        for m, a, n in pieces[4:5]:
             largest(pooled[m][:, a // D : (a + n) // D], accs[m, a][:])
-        bias_relu(1, result[1][:, : V // 2], pooled[1][:, : V // 2])
-        store(0, 3 * V // 2)
-        for m, a, n in pieces[6:]:
+        bias_relu(1, result[1][:, : V // 4], pooled[1][:, : V // 4])
+        store(0, 5 * V // 4)
+        for m, a, n in pieces[5:]:
             largest(pooled[m][:, a // D : (a + n) // D], accs[m, a][:])
         nc.vector.tensor_scalar(
-            out=result[1][:, V // 2 :], in0=pooled[1][:, V // 2 :],
+            out=result[1][:, V // 4 :], in0=pooled[1][:, V // 4 :],
             scalar1=bias[:, 1:2], scalar2=0.0, op0=ADD, op1=MAX,
         )
-        store(3 * V // 2, 2 * V)
+        store(5 * V // 4, 2 * V)

@@ -13,6 +13,7 @@ U32 = mybir.dt.uint32
 U16 = mybir.dt.uint16
 U8 = mybir.dt.uint8
 FP8X4 = mybir.dt.float8_e4m3fn_x4
+COPY = mybir.ActivationFunctionType.Copy
 RELU = mybir.ActivationFunctionType.Relu
 IDENTITY = mybir.ActivationFunctionType.Identity
 ADD = mybir.AluOpType.add
@@ -22,6 +23,8 @@ AXIS_X = mybir.AxisListType.X
 HALF = S // 2
 QUARTER = S // 4
 LIST_COLS = S // 16
+W_FIRST = 32
+W_SCALAR = 64
 
 
 def tile_picked_pool_lin_relu_sub_e_kernel(tc, xT, w, b, offs, out):
@@ -33,86 +36,64 @@ def tile_picked_pool_lin_relu_sub_e_kernel(tc, xT, w, b, offs, out):
         offsets = keep.tile([P, LIST_COLS], U16, name="offsets")
         first_pair = keep.tile([P, 2, T], F32, name="first_pair", align_bytes=64)
         planes = {t: keep.tile([P, T], F32, name=f"plane{t}", align_bytes=64) for t in (2, 3)}
-        picked_pair = [keep.tile([P, 2, HALF], F32, name=f"picked_pair{h}", align_bytes=64) for h in range(2)]
+        picked_first = [keep.tile([P, 2, HALF], F32, name=f"picked_first{h}", align_bytes=64) for h in range(2)]
+        picked_last = [keep.tile([P, 2, QUARTER], F32, name=f"picked_last{q}", align_bytes=64) for q in range(2)]
         w_raw = keep.tile([P, PACK, N], F32, name="w_raw", align_bytes=64)
-        zeros = keep.tile([P, 64], F32, name="zeros", tag="rows_then_scales", align_bytes=64)
+        zeros = [keep.tile([P, 64], F32, name=f"zeros{i}", tag=f"zeros_then_scales{i}", align_bytes=64) for i in range(2)]
         bias = keep.tile([P, 2], F32, name="bias", align_bytes=64)
-        x_grouped = [keep.tile([P, HALF, PACK], BF16, name=f"x_grouped{h}", align_bytes=64) for h in range(2)]
+        first_half = keep.tile([P, HALF, PACK], BF16, name="first_half", align_bytes=64)
+        late_quarters = [keep.tile([P, QUARTER, PACK], BF16, name=f"late_quarter{q}", align_bytes=64) for q in range(2)]
         x_codes = keep.tile([P, S], U32, name="x_codes", align_bytes=64)
-        x_scales = [keep.tile([P, HALF], U8, name="x_scales0", align_bytes=64)]
+        first_scales = keep.tile([P, QUARTER], U8, name="first_scales", align_bytes=64)
         w_grouped = [keep.tile([P, P, PACK], BF16, name=f"w_grouped{h}", align_bytes=64) for h in range(2)]
         w_codes = keep.tile([P, N], U32, name="w_codes", align_bytes=64)
         w_scales = keep.tile([P, N], U8, name="w_scales", align_bytes=64)
-        pieces = [(m, q * QUARTER, QUARTER) for m in range(2) for q in range(4)]
-        accs = {(m, a): psum.tile([P, n], F32, name=f"acc{m}_{a}") for m, a, n in pieces}
-        pooled = [keep.tile([P, V], F32, name=f"pooled{h}") for h in range(2)]
+        accs = {(m, q): psum.tile([P, QUARTER], F32, name=f"acc{m}_{q}") for m in range(2) for q in range(4)}
+        pooled = [keep.tile([P, V], F32, name=f"pooled{m}") for m in range(2)]
         results = keep.tile([P, 2, V], F32, name="results")
-        result = [results[:, h, :] for h in range(2)]
 
         x_rows = xT.rearrange("(p j) t -> p j t", j=PACK)
-        lcols = [slice(h * LIST_COLS // 2, (h + 1) * LIST_COLS // 2) for h in range(2)]
-        cols = [slice(h * HALF, (h + 1) * HALF) for h in range(2)]
-        mcols = [slice(h * P, (h + 1) * P) for h in range(2)]
-        w_rows = w.rearrange("(p j) m -> p j m", j=PACK)
         nc.sync.dma_start(first_pair[:], x_rows[:, 0:2, :])
         nc.sync.dma_start(offsets[:], offs)
-        nc.vector.memset(zeros[:, 0:1], 0.0)
+        for i in range(2):
+            nc.vector.memset(zeros[i][:, 0:1], 0.0)
         nc.sync.dma_start(planes[2][:], x_rows[:, 2, :])
         nc.sync.dma_start(planes[3][:], x_rows[:, 3, :])
-        nc.sync.dma_start(w_raw[:], w_rows)
+        nc.sync.dma_start(w_raw[:], w.rearrange("(p j) m -> p j m", j=PACK))
         nc.sync.dma_start(bias[:], b.rearrange("(p h) o -> p (h o)", h=2))
 
-        def gather(h, t):
-            nc.vector.tensor_copy(x_grouped[h][:, :, t], planes[t][:].indirect(offsets[:, lcols[h]]))
+        def entries(a, n):
+            return offsets[:, a // 16 : (a + n) // 16]
 
-        def gather_plain(h, t):
-            nc.vector.tensor_copy(picked_pair[h][:, t, :], first_pair[:, t, :].indirect(offsets[:, lcols[h]]))
+        def weight_views(m, a, z):
+            dst = w_grouped[m][:, a:z, :].rearrange("p (c i) j -> p c j i", i=4)
+            src = w_raw[:, :, 2 * a : 2 * z].rearrange("p j (c i h) -> p h c j i", i=4, h=2)[:, m]
+            return dst, src
 
-        def weave_pair(h):
-            nc.scalar.copy(x_grouped[h][:, :, 0:2], picked_pair[h][:].rearrange("p j n -> p n j"))
+        def quantize(codes, scales, grouped):
+            nc.vector.quantize_mx(out=codes.bitcast(FP8X4), scales=scales, in_=grouped.rearrange("p n j -> p (n j)"))
 
-        def quantize_x(h):
-            nc.vector.quantize_mx(
-                out=x_codes[:, cols[h]].bitcast(FP8X4),
-                scales=x_scales[h][:],
-                in_=x_grouped[h][:].rearrange("p n j -> p (n j)"),
-            )
+        def quantize_w(m):
+            quantize(w_codes[:, m * P : (m + 1) * P], w_scales[:, m * P : (m + 1) * P], w_grouped[m][:])
 
-        def quantize_w(h):
-            nc.vector.quantize_mx(
-                out=w_codes[:, mcols[h]].bitcast(FP8X4),
-                scales=w_scales[:, mcols[h]],
-                in_=w_grouped[h][:].rearrange("p n j -> p (n j)"),
-            )
-
-        def product(m, a, n):
+        def product(m, q):
             nc.tensor.matmul_mx(
-                out=accs[m, a][:],
-                lhsT=w_codes[:, mcols[m]].bitcast(FP8X4),
-                lhsT_scale=w_scales[:, mcols[m]],
-                rhs=x_codes[:, a : a + n].bitcast(FP8X4),
-                rhs_scale=x_scales[a // HALF][:, a % HALF : a % HALF + n],
+                out=accs[m, q][:],
+                lhsT=w_codes[:, m * P : (m + 1) * P].bitcast(FP8X4),
+                lhsT_scale=w_scales[:, m * P : (m + 1) * P],
+                rhs=x_codes[:, q * QUARTER : (q + 1) * QUARTER].bitcast(FP8X4),
+                rhs_scale=x_scales[q],
                 start=True,
                 stop=True,
             )
 
-        def w_copy_s(m):
-            nc.scalar.copy(
-                w_grouped[m][:].rearrange("p (c i) j -> p c j i", i=4),
-                w_raw[:].rearrange("p j (c i h) -> p h c j i", i=4, h=2)[:, m],
+        def largest(m, q):
+            nc.vector.tensor_reduce(
+                out=pooled[m][:, q * QUARTER // D : (q + 1) * QUARTER // D],
+                in_=accs[m, q][:].rearrange("p (v d) -> p v d", d=D),
+                axis=AXIS_X,
+                op=MAX,
             )
-
-        def largest(dst, src):
-            nc.vector.tensor_reduce(out=dst, in_=src.rearrange("p (v d) -> p v d", d=D), axis=AXIS_X, op=MAX)
-
-        def bias_relu(m, dst, src):
-            nc.scalar.activation(dst, src, RELU, bias=bias[:, m : m + 1])
-
-        def pool_then_finish(m, a, n):
-            v = slice(a // D, (a + n) // D)
-            largest(pooled[m][:, v], accs[m, a][:])
-            bias_relu(m, result[m][:, v], pooled[m][:, v])
-
 
         def store(a, z):
             nc.sync.dma_start(
@@ -121,43 +102,47 @@ def tile_picked_pool_lin_relu_sub_e_kernel(tc, xT, w, b, offs, out):
             )
 
         for h in range(2):
-            gather_plain(h, 0)
-            gather_plain(h, 1)
-        weave_pair(0)
-        gather(1, 2)
-        weave_pair(1)
-        gather(0, 2)
-        for h in range(2):
-            gather(h, 3)
-        nc.scalar.activation(
-            w_grouped[0][:].rearrange("p (c i) j -> p c j i", i=4),
-            w_raw[:].rearrange("p j (c i h) -> p h c j i", i=4, h=2)[:, 0],
-            IDENTITY,
-            bias=zeros[:, 0:1],
-        )
-        w_copy_s(1)
-        x_scales.append(keep.tile([P, HALF], U8, name="x_scales1", tag="rows_then_scales", align_bytes=64))
-        quantize_x(0)
+            for t in range(2):
+                nc.vector.tensor_copy(picked_first[h][:, t, :], first_pair[:, t, :].indirect(entries(h * HALF, HALF)))
+        nc.scalar.copy(first_half[:, :, 0:2], picked_first[0][:].rearrange("p j n -> p n j"))
+        for q in range(2):
+            nc.scalar.copy(
+                late_quarters[q][:, :, 0:2],
+                picked_first[1][:, :, q * QUARTER : (q + 1) * QUARTER].rearrange("p j n -> p n j"),
+            )
+        for q in range(2):
+            nc.vector.tensor_copy(picked_last[q][:, 0, :], planes[2][:].indirect(entries(HALF + q * QUARTER, QUARTER)))
+        nc.vector.tensor_copy(first_half[:, :, 2], planes[2][:].indirect(entries(0, HALF)))
+        nc.vector.tensor_copy(first_half[:, :, 3], planes[3][:].indirect(entries(0, HALF)))
+        for q in range(2):
+            nc.scalar.activation(picked_last[q][:, 1, :], planes[3][:].indirect(entries(HALF + q * QUARTER, QUARTER)), COPY)
+        nc.scalar.copy(late_quarters[0][:, :, 2:4], picked_last[0][:].rearrange("p j n -> p n j"))
+        nc.vector.tensor_copy(late_quarters[1][:, :, 2:4], picked_last[1][:].rearrange("p j n -> p n j"))
+        quantize(x_codes[:, :QUARTER], first_scales[:], first_half[:, :QUARTER, :])
+        nc.scalar.activation(*weight_views(0, 0, W_FIRST), IDENTITY, bias=zeros[0][:, 0:1])
+        nc.scalar.activation(*weight_views(0, W_FIRST, W_SCALAR), IDENTITY, bias=zeros[1][:, 0:1])
+        nc.vector.tensor_copy(*weight_views(0, W_SCALAR, P))
+        nc.scalar.copy(*weight_views(1, 0, P))
+        second_scales = keep.tile([P, QUARTER], U8, name="second_scales", tag="zeros_then_scales0", align_bytes=64)
+        half_scales = keep.tile([P, HALF], U8, name="half_scales", tag="zeros_then_scales1", align_bytes=64)
+        x_scales = [first_scales[:], second_scales[:], half_scales[:, :QUARTER], half_scales[:, QUARTER:]]
+        quantize(x_codes[:, QUARTER:HALF], second_scales[:], first_half[:, QUARTER:, :])
         quantize_w(0)
-        product(*pieces[0])
-        product(*pieces[1])
-        quantize_x(1)
-        product(*pieces[2])
-        product(*pieces[3])
+        for q in range(2):
+            quantize(x_codes[:, (2 + q) * QUARTER : (3 + q) * QUARTER], x_scales[2 + q], late_quarters[q][:])
         quantize_w(1)
-        for piece in pieces[4:]:
-            product(*piece)
-        for m, a, n in pieces[:4]:
-            largest(pooled[m][:, a // D : (a + n) // D], accs[m, a][:])
-        bias_relu(0, result[0][:], pooled[0][:])
-        for m, a, n in pieces[4:5]:
-            largest(pooled[m][:, a // D : (a + n) // D], accs[m, a][:])
-        bias_relu(1, result[1][:, : V // 4], pooled[1][:, : V // 4])
+        for m in range(2):
+            for q in range(4):
+                product(m, q)
+        for q in range(4):
+            largest(0, q)
+        nc.scalar.activation(results[:, 0, :], pooled[0][:], RELU, bias=bias[:, 0:1])
+        largest(1, 0)
+        nc.scalar.activation(results[:, 1, : V // 4], pooled[1][:, : V // 4], RELU, bias=bias[:, 1:2])
         store(0, 5 * V // 4)
-        for m, a, n in pieces[5:]:
-            largest(pooled[m][:, a // D : (a + n) // D], accs[m, a][:])
+        for q in range(1, 4):
+            largest(1, q)
         nc.vector.tensor_scalar(
-            out=result[1][:, V // 4 :], in0=pooled[1][:, V // 4 :],
-            scalar1=bias[:, 1:2], scalar2=0.0, op0=ADD, op1=MAX,
+            out=results[:, 1, V // 4 :], in0=pooled[1][:, V // 4 :], scalar1=bias[:, 1:2], scalar2=0.0, op0=ADD, op1=MAX
         )
         store(5 * V // 4, 2 * V)

@@ -23,8 +23,9 @@ AXIS_X = mybir.AxisListType.X
 HALF = S // 2
 QUARTER = S // 4
 LIST_COLS = S // 16
-W_FIRST = 32
-W_SCALAR = 64
+BY_VECTOR = S - QUARTER
+W_FIRST = 16
+W_SCALAR = 48
 
 
 def tile_picked_pool_lin_relu_sub_e_kernel(tc, xT, w, b, offs, out):
@@ -37,14 +38,13 @@ def tile_picked_pool_lin_relu_sub_e_kernel(tc, xT, w, b, offs, out):
         first_pair = keep.tile([P, 2, T], F32, name="first_pair", align_bytes=64)
         planes = {t: keep.tile([P, T], F32, name=f"plane{t}", align_bytes=64) for t in (2, 3)}
         picked_first = [keep.tile([P, 2, HALF], F32, name=f"picked_first{h}", align_bytes=64) for h in range(2)]
-        picked_last = [keep.tile([P, 2, QUARTER], F32, name=f"picked_last{q}", align_bytes=64) for q in range(2)]
+        picked_last = keep.tile([P, 2, QUARTER], F32, name="picked_last", align_bytes=64)
         w_raw = keep.tile([P, PACK, N], F32, name="w_raw", align_bytes=64)
         zeros = [keep.tile([P, 64], F32, name=f"zeros{i}", tag=f"zeros_then_scales{i}", align_bytes=64) for i in range(2)]
         bias = keep.tile([P, 2], F32, name="bias", align_bytes=64)
-        first_half = keep.tile([P, HALF, PACK], BF16, name="first_half", align_bytes=64)
-        late_quarters = [keep.tile([P, QUARTER, PACK], BF16, name=f"late_quarter{q}", align_bytes=64) for q in range(2)]
+        x_early = keep.tile([P, BY_VECTOR, PACK], BF16, name="x_early", align_bytes=64)
+        x_late = keep.tile([P, QUARTER, PACK], BF16, name="x_late", align_bytes=64)
         x_codes = keep.tile([P, S], U32, name="x_codes", align_bytes=64)
-        first_scales = keep.tile([P, QUARTER], U8, name="first_scales", align_bytes=64)
         w_grouped = [keep.tile([P, P, PACK], BF16, name=f"w_grouped{h}", align_bytes=64) for h in range(2)]
         w_codes = keep.tile([P, N], U32, name="w_codes", align_bytes=64)
         w_scales = keep.tile([P, N], U8, name="w_scales", align_bytes=64)
@@ -82,7 +82,7 @@ def tile_picked_pool_lin_relu_sub_e_kernel(tc, xT, w, b, offs, out):
                 lhsT=w_codes[:, m * P : (m + 1) * P].bitcast(FP8X4),
                 lhsT_scale=w_scales[:, m * P : (m + 1) * P],
                 rhs=x_codes[:, q * QUARTER : (q + 1) * QUARTER].bitcast(FP8X4),
-                rhs_scale=x_scales[q],
+                rhs_scale=x_scales[q // 2][:, q % 2 * QUARTER : (q % 2 + 1) * QUARTER],
                 start=True,
                 stop=True,
             )
@@ -101,35 +101,31 @@ def tile_picked_pool_lin_relu_sub_e_kernel(tc, xT, w, b, offs, out):
                 results[:].rearrange("p m v -> p (m v)")[:, a:z],
             )
 
+        def pairs(picked):
+            return picked.rearrange("p j n -> p n j")
+
         for h in range(2):
             for t in range(2):
                 nc.vector.tensor_copy(picked_first[h][:, t, :], first_pair[:, t, :].indirect(entries(h * HALF, HALF)))
-        nc.scalar.copy(first_half[:, :, 0:2], picked_first[0][:].rearrange("p j n -> p n j"))
-        for q in range(2):
-            nc.scalar.copy(
-                late_quarters[q][:, :, 0:2],
-                picked_first[1][:, :, q * QUARTER : (q + 1) * QUARTER].rearrange("p j n -> p n j"),
-            )
-        for q in range(2):
-            nc.vector.tensor_copy(picked_last[q][:, 0, :], planes[2][:].indirect(entries(HALF + q * QUARTER, QUARTER)))
-        nc.vector.tensor_copy(first_half[:, :, 2], planes[2][:].indirect(entries(0, HALF)))
-        nc.vector.tensor_copy(first_half[:, :, 3], planes[3][:].indirect(entries(0, HALF)))
-        for q in range(2):
-            nc.scalar.activation(picked_last[q][:, 1, :], planes[3][:].indirect(entries(HALF + q * QUARTER, QUARTER)), COPY)
-        nc.scalar.copy(late_quarters[0][:, :, 2:4], picked_last[0][:].rearrange("p j n -> p n j"))
-        nc.vector.tensor_copy(late_quarters[1][:, :, 2:4], picked_last[1][:].rearrange("p j n -> p n j"))
-        quantize(x_codes[:, :QUARTER], first_scales[:], first_half[:, :QUARTER, :])
+        nc.scalar.copy(x_early[:, :HALF, 0:2], pairs(picked_first[0][:]))
+        nc.scalar.copy(x_early[:, HALF:, 0:2], pairs(picked_first[1][:, :, :QUARTER]))
+        nc.scalar.copy(x_late[:, :, 0:2], pairs(picked_first[1][:, :, QUARTER:]))
+        nc.vector.tensor_copy(picked_last[:, 0, :], planes[2][:].indirect(entries(BY_VECTOR, QUARTER)))
+        for t in (2, 3):
+            nc.vector.tensor_copy(x_early[:, :, t], planes[t][:].indirect(entries(0, BY_VECTOR)))
+        nc.scalar.activation(picked_last[:, 1, :], planes[3][:].indirect(entries(BY_VECTOR, QUARTER)), COPY)
+        nc.scalar.copy(x_late[:, :, 2:4], pairs(picked_last[:]))
         nc.scalar.activation(*weight_views(0, 0, W_FIRST), IDENTITY, bias=zeros[0][:, 0:1])
         nc.scalar.activation(*weight_views(0, W_FIRST, W_SCALAR), IDENTITY, bias=zeros[1][:, 0:1])
         nc.vector.tensor_copy(*weight_views(0, W_SCALAR, P))
         nc.scalar.copy(*weight_views(1, 0, P))
-        second_scales = keep.tile([P, QUARTER], U8, name="second_scales", tag="zeros_then_scales0", align_bytes=64)
-        half_scales = keep.tile([P, HALF], U8, name="half_scales", tag="zeros_then_scales1", align_bytes=64)
-        x_scales = [first_scales[:], second_scales[:], half_scales[:, :QUARTER], half_scales[:, QUARTER:]]
-        quantize(x_codes[:, QUARTER:HALF], second_scales[:], first_half[:, QUARTER:, :])
+        x_scales = [
+            keep.tile([P, HALF], U8, name=f"x_scales{h}", tag=f"zeros_then_scales{h}", align_bytes=64) for h in range(2)
+        ]
+        quantize(x_codes[:, :HALF], x_scales[0][:], x_early[:, :HALF, :])
         quantize_w(0)
-        for q in range(2):
-            quantize(x_codes[:, (2 + q) * QUARTER : (3 + q) * QUARTER], x_scales[2 + q], late_quarters[q][:])
+        quantize(x_codes[:, HALF:BY_VECTOR], x_scales[1][:, :QUARTER], x_early[:, HALF:, :])
+        quantize(x_codes[:, BY_VECTOR:], x_scales[1][:, QUARTER:], x_late[:])
         quantize_w(1)
         for m in range(2):
             for q in range(4):

@@ -23,9 +23,10 @@ AXIS_X = mybir.AxisListType.X
 HALF = S // 2
 QUARTER = S // 4
 LIST_COLS = S // 16
+EIGHTH = S // 8
 BY_VECTOR = S - QUARTER
-W_FIRST = 16
-W_SCALAR = 48
+W_FIRST = 4
+W_SCALAR = 32
 
 
 def tile_picked_pool_lin_relu_sub_e_kernel(tc, xT, w, b, offs, out):
@@ -38,7 +39,7 @@ def tile_picked_pool_lin_relu_sub_e_kernel(tc, xT, w, b, offs, out):
         first_pair = keep.tile([P, 2, T], F32, name="first_pair", align_bytes=64)
         planes = {t: keep.tile([P, T], F32, name=f"plane{t}", align_bytes=64) for t in (2, 3)}
         picked_first = [keep.tile([P, 2, HALF], F32, name=f"picked_first{h}", align_bytes=64) for h in range(2)]
-        picked_last = keep.tile([P, 2, QUARTER], F32, name="picked_last", align_bytes=64)
+        picked_last = [keep.tile([P, 2, EIGHTH], F32, name=f"picked_last{e}", align_bytes=64) for e in range(2)]
         w_raw = keep.tile([P, PACK, N], F32, name="w_raw", align_bytes=64)
         zeros = [keep.tile([P, 64], F32, name=f"zeros{i}", tag=f"zeros_then_scales{i}", align_bytes=64) for i in range(2)]
         bias = keep.tile([P, 2], F32, name="bias", align_bytes=64)
@@ -110,11 +111,14 @@ def tile_picked_pool_lin_relu_sub_e_kernel(tc, xT, w, b, offs, out):
         nc.scalar.copy(x_early[:, :HALF, 0:2], pairs(picked_first[0][:]))
         nc.scalar.copy(x_early[:, HALF:, 0:2], pairs(picked_first[1][:, :, :QUARTER]))
         nc.scalar.copy(x_late[:, :, 0:2], pairs(picked_first[1][:, :, QUARTER:]))
-        nc.vector.tensor_copy(picked_last[:, 0, :], planes[2][:].indirect(entries(BY_VECTOR, QUARTER)))
+        for e in range(2):
+            nc.scalar.activation(picked_last[e][:, 0, :], planes[2][:].indirect(entries(BY_VECTOR + e * EIGHTH, EIGHTH)), COPY)
         for t in (2, 3):
             nc.vector.tensor_copy(x_early[:, :, t], planes[t][:].indirect(entries(0, BY_VECTOR)))
-        nc.scalar.activation(picked_last[:, 1, :], planes[3][:].indirect(entries(BY_VECTOR, QUARTER)), COPY)
-        nc.scalar.copy(x_late[:, :, 2:4], pairs(picked_last[:]))
+        for e in range(2):
+            nc.scalar.activation(picked_last[e][:, 1, :], planes[3][:].indirect(entries(BY_VECTOR + e * EIGHTH, EIGHTH)), COPY)
+        for e in range(2):
+            nc.scalar.copy(x_late[:, e * EIGHTH : (e + 1) * EIGHTH, 2:4], pairs(picked_last[e][:]))
         nc.scalar.activation(*weight_views(0, 0, W_FIRST), IDENTITY, bias=zeros[0][:, 0:1])
         nc.scalar.activation(*weight_views(0, W_FIRST, W_SCALAR), IDENTITY, bias=zeros[1][:, 0:1])
         nc.vector.tensor_copy(*weight_views(0, W_SCALAR, P))

@@ -26,7 +26,7 @@ LIST_COLS = S // 16
 EIGHTH = S // 8
 BY_VECTOR = S - QUARTER
 W_FIRST = 4
-W_SCALAR = 32
+W_SCALAR = 88
 
 
 def tile_picked_pool_lin_relu_sub_e_kernel(tc, xT, w, b, offs, out):

@@ -23,8 +23,8 @@ AXIS_X = mybir.AxisListType.X
 HALF = S // 2
 QUARTER = S // 4
 LIST_COLS = S // 16
-EIGHTH = S // 8
-BY_VECTOR = S - QUARTER
+SCALAR_PIECES = (64, 64)
+BY_VECTOR = S - sum(SCALAR_PIECES)
 W_FIRST = 4
 W_SCALAR = 88
 
@@ -39,12 +39,14 @@ def tile_picked_pool_lin_relu_sub_e_kernel(tc, xT, w, b, offs, out):
         first_pair = keep.tile([P, 2, T], F32, name="first_pair", align_bytes=64)
         planes = {t: keep.tile([P, T], F32, name=f"plane{t}", align_bytes=64) for t in (2, 3)}
         picked_first = [keep.tile([P, 2, HALF], F32, name=f"picked_first{h}", align_bytes=64) for h in range(2)]
-        picked_last = [keep.tile([P, 2, EIGHTH], F32, name=f"picked_last{e}", align_bytes=64) for e in range(2)]
+        starts = [BY_VECTOR + sum(SCALAR_PIECES[:e]) for e in range(len(SCALAR_PIECES))]
+        picked_last = [
+            keep.tile([P, 2, n], F32, name=f"picked_last{e}", align_bytes=64) for e, n in enumerate(SCALAR_PIECES)
+        ]
         w_raw = keep.tile([P, PACK, N], F32, name="w_raw", align_bytes=64)
         zeros = [keep.tile([P, 64], F32, name=f"zeros{i}", tag=f"zeros_then_scales{i}", align_bytes=64) for i in range(2)]
         bias = keep.tile([P, 2], F32, name="bias", align_bytes=64)
-        x_early = keep.tile([P, BY_VECTOR, PACK], BF16, name="x_early", align_bytes=64)
-        x_late = keep.tile([P, QUARTER, PACK], BF16, name="x_late", align_bytes=64)
+        x_grouped = keep.tile([P, S, PACK], BF16, name="x_grouped", align_bytes=64)
         x_codes = keep.tile([P, S], U32, name="x_codes", align_bytes=64)
         w_grouped = [keep.tile([P, P, PACK], BF16, name=f"w_grouped{h}", align_bytes=64) for h in range(2)]
         w_codes = keep.tile([P, N], U32, name="w_codes", align_bytes=64)
@@ -83,7 +85,7 @@ def tile_picked_pool_lin_relu_sub_e_kernel(tc, xT, w, b, offs, out):
                 lhsT=w_codes[:, m * P : (m + 1) * P].bitcast(FP8X4),
                 lhsT_scale=w_scales[:, m * P : (m + 1) * P],
                 rhs=x_codes[:, q * QUARTER : (q + 1) * QUARTER].bitcast(FP8X4),
-                rhs_scale=x_scales[q // 2][:, q % 2 * QUARTER : (q % 2 + 1) * QUARTER],
+                rhs_scale=x_scales[q],
                 start=True,
                 stop=True,
             )
@@ -108,33 +110,43 @@ def tile_picked_pool_lin_relu_sub_e_kernel(tc, xT, w, b, offs, out):
         for h in range(2):
             for t in range(2):
                 nc.vector.tensor_copy(picked_first[h][:, t, :], first_pair[:, t, :].indirect(entries(h * HALF, HALF)))
-        nc.scalar.copy(x_early[:, :HALF, 0:2], pairs(picked_first[0][:]))
-        nc.scalar.copy(x_early[:, HALF:, 0:2], pairs(picked_first[1][:, :, :QUARTER]))
-        nc.scalar.copy(x_late[:, :, 0:2], pairs(picked_first[1][:, :, QUARTER:]))
-        for e in range(2):
-            nc.scalar.activation(picked_last[e][:, 0, :], planes[2][:].indirect(entries(BY_VECTOR + e * EIGHTH, EIGHTH)), COPY)
+        for h in range(2):
+            nc.scalar.copy(x_grouped[:, h * HALF : (h + 1) * HALF, 0:2], pairs(picked_first[h][:]))
         for t in (2, 3):
-            nc.vector.tensor_copy(x_early[:, :, t], planes[t][:].indirect(entries(0, BY_VECTOR)))
-        for e in range(2):
-            nc.scalar.activation(picked_last[e][:, 1, :], planes[3][:].indirect(entries(BY_VECTOR + e * EIGHTH, EIGHTH)), COPY)
-        for e in range(2):
-            nc.scalar.copy(x_late[:, e * EIGHTH : (e + 1) * EIGHTH, 2:4], pairs(picked_last[e][:]))
+            nc.vector.tensor_copy(x_grouped[:, :BY_VECTOR, t], planes[t][:].indirect(entries(0, BY_VECTOR)))
+            for picked, a, n in zip(picked_last, starts, SCALAR_PIECES):
+                nc.scalar.activation(picked[:, t - 2, :], planes[t][:].indirect(entries(a, n)), COPY)
+        for picked, a, n in zip(picked_last, starts, SCALAR_PIECES):
+            nc.scalar.copy(x_grouped[:, a : a + n, 2:4], pairs(picked[:]))
         nc.scalar.activation(*weight_views(0, 0, W_FIRST), IDENTITY, bias=zeros[0][:, 0:1])
         nc.scalar.activation(*weight_views(0, W_FIRST, W_SCALAR), IDENTITY, bias=zeros[1][:, 0:1])
         nc.vector.tensor_copy(*weight_views(0, W_SCALAR, P))
         nc.scalar.copy(*weight_views(1, 0, P))
+        outer_scales = keep.tile([P, HALF], U8, name="outer_scales", tag="zeros_then_scales0", align_bytes=64)
+        middle_scales = keep.tile([P, HALF], U8, name="middle_scales", tag="zeros_then_scales1", align_bytes=64)
         x_scales = [
-            keep.tile([P, HALF], U8, name=f"x_scales{h}", tag=f"zeros_then_scales{h}", align_bytes=64) for h in range(2)
+            outer_scales[:, :QUARTER],
+            middle_scales[:, :QUARTER],
+            middle_scales[:, QUARTER:],
+            outer_scales[:, QUARTER:],
         ]
-        quantize(x_codes[:, :HALF], x_scales[0][:], x_early[:, :HALF, :])
+
+        def quantize_x(q):
+            cols = slice(q * QUARTER, (q + 1) * QUARTER)
+            quantize(x_codes[:, cols], x_scales[q], x_grouped[:, cols, :])
+
+        quantize_x(3)
+        quantize_x(0)
         quantize_w(0)
-        quantize(x_codes[:, HALF:BY_VECTOR], x_scales[1][:, :QUARTER], x_early[:, HALF:, :])
-        quantize(x_codes[:, BY_VECTOR:], x_scales[1][:, QUARTER:], x_late[:])
+        quantize_x(1)
+        quantize_x(2)
         quantize_w(1)
-        for m in range(2):
-            for q in range(4):
-                product(m, q)
+        ready_order = (0, 3, 1, 2)
+        for q in ready_order:
+            product(0, q)
         for q in range(4):
+            product(1, q)
+        for q in ready_order:
             largest(0, q)
         nc.scalar.activation(results[:, 0, :], pooled[0][:], RELU, bias=bias[:, 0:1])
         largest(1, 0)

@@ -38,10 +38,11 @@ def tile_picked_pool_lin_relu_sub_e_kernel(tc, xT, w, b, offs, out):
         offsets = keep.tile([P, LIST_COLS], U16, name="offsets")
         first_pair = keep.tile([P, 2, T], F32, name="first_pair", align_bytes=64)
         planes = {t: keep.tile([P, T], F32, name=f"plane{t}", align_bytes=64) for t in (2, 3)}
-        picked_first = [keep.tile([P, 2, HALF], F32, name=f"picked_first{h}", align_bytes=64) for h in range(2)]
+        picked_half = keep.tile([P, 2, HALF], F32, name="picked_half", align_bytes=64)
+        picked_rest = keep.tile([P, 3, HALF], F32, name="picked_rest", align_bytes=64)
         starts = [BY_VECTOR + sum(SCALAR_PIECES[:e]) for e in range(len(SCALAR_PIECES))]
         picked_last = [
-            keep.tile([P, 2, n], F32, name=f"picked_last{e}", align_bytes=64) for e, n in enumerate(SCALAR_PIECES)
+            keep.tile([P, n], F32, name=f"picked_last{e}", align_bytes=64) for e, n in enumerate(SCALAR_PIECES)
         ]
         w_raw = keep.tile([P, PACK, N], F32, name="w_raw", align_bytes=64)
         zeros = [keep.tile([P, 64], F32, name=f"zeros{i}", tag=f"zeros_then_scales{i}", align_bytes=64) for i in range(2)]
@@ -107,17 +108,21 @@ def tile_picked_pool_lin_relu_sub_e_kernel(tc, xT, w, b, offs, out):
         def pairs(picked):
             return picked.rearrange("p j n -> p n j")
 
-        for h in range(2):
+        for h, picked in enumerate((picked_half, picked_rest)):
             for t in range(2):
-                nc.vector.tensor_copy(picked_first[h][:, t, :], first_pair[:, t, :].indirect(entries(h * HALF, HALF)))
-        for h in range(2):
-            nc.scalar.copy(x_grouped[:, h * HALF : (h + 1) * HALF, 0:2], pairs(picked_first[h][:]))
-        for t in (2, 3):
-            nc.vector.tensor_copy(x_grouped[:, :BY_VECTOR, t], planes[t][:].indirect(entries(0, BY_VECTOR)))
-            for picked, a, n in zip(picked_last, starts, SCALAR_PIECES):
-                nc.scalar.activation(picked[:, t - 2, :], planes[t][:].indirect(entries(a, n)), COPY)
+                nc.vector.tensor_copy(picked[:, t, :], first_pair[:, t, :].indirect(entries(h * HALF, HALF)))
+        nc.scalar.copy(x_grouped[:, :HALF, 0:2], pairs(picked_half[:]))
+        by_vector = BY_VECTOR - HALF
+        nc.vector.tensor_copy(picked_rest[:, 2, :by_vector], planes[2][:].indirect(entries(HALF, by_vector)))
+        nc.vector.tensor_copy(x_grouped[:, :HALF, 2], planes[2][:].indirect(entries(0, HALF)))
+        nc.vector.tensor_copy(x_grouped[:, HALF:BY_VECTOR, 0:3], pairs(picked_rest[:, :, :by_vector]))
+        nc.scalar.activation(picked_rest[:, 2, by_vector:], planes[2][:].indirect(entries(BY_VECTOR, S - BY_VECTOR)), COPY)
+        nc.scalar.copy(x_grouped[:, BY_VECTOR:, 0:3], pairs(picked_rest[:, :, by_vector:]))
+        nc.vector.tensor_copy(x_grouped[:, :BY_VECTOR, 3], planes[3][:].indirect(entries(0, BY_VECTOR)))
         for picked, a, n in zip(picked_last, starts, SCALAR_PIECES):
-            nc.scalar.copy(x_grouped[:, a : a + n, 2:4], pairs(picked[:]))
+            nc.scalar.activation(picked[:], planes[3][:].indirect(entries(a, n)), COPY)
+        for picked, a, n in zip(picked_last, starts, SCALAR_PIECES):
+            nc.scalar.copy(x_grouped[:, a : a + n, 3], picked[:])
         nc.scalar.activation(*weight_views(0, 0, W_FIRST), IDENTITY, bias=zeros[0][:, 0:1])
         nc.scalar.activation(*weight_views(0, W_FIRST, W_SCALAR), IDENTITY, bias=zeros[1][:, 0:1])
         nc.vector.tensor_copy(*weight_views(0, W_SCALAR, P))

@@ -22,11 +22,10 @@ AXIS_X = mybir.AxisListType.X
 
 HALF = S // 2
 QUARTER = S // 4
+EIGHTH = S // 8
 LIST_COLS = S // 16
-SCALAR_PIECES = (64, 64)
-BY_VECTOR = S - sum(SCALAR_PIECES)
 W_FIRST = 4
-W_SCALAR = 88
+W_SCALAR = 64
 
 
 def tile_picked_pool_lin_relu_sub_e_kernel(tc, xT, w, b, offs, out):
@@ -40,14 +39,15 @@ def tile_picked_pool_lin_relu_sub_e_kernel(tc, xT, w, b, offs, out):
         planes = {t: keep.tile([P, T], F32, name=f"plane{t}", align_bytes=64) for t in (2, 3)}
         picked_half = keep.tile([P, 2, HALF], F32, name="picked_half", align_bytes=64)
         picked_rest = keep.tile([P, 3, HALF], F32, name="picked_rest", align_bytes=64)
-        starts = [BY_VECTOR + sum(SCALAR_PIECES[:e]) for e in range(len(SCALAR_PIECES))]
-        picked_last = [
-            keep.tile([P, n], F32, name=f"picked_last{e}", align_bytes=64) for e, n in enumerate(SCALAR_PIECES)
-        ]
+        picked_third = keep.tile([P, QUARTER], F32, name="picked_third", align_bytes=64)
+        picked_last = [keep.tile([P, EIGHTH], F32, name=f"picked_last{e}", align_bytes=64) for e in range(2)]
         w_raw = keep.tile([P, PACK, N], F32, name="w_raw", align_bytes=64)
-        zeros = [keep.tile([P, 64], F32, name=f"zeros{i}", tag=f"zeros_then_scales{i}", align_bytes=64) for i in range(2)]
+        one = keep.tile([P, 64], F32, name="one", tag="one_then_scales", align_bytes=64)
+        zero = keep.tile([P, 96], F32, name="zero", tag="zero_then_scales", align_bytes=64)
         bias = keep.tile([P, 2], F32, name="bias", align_bytes=64)
-        x_grouped = keep.tile([P, S, PACK], BF16, name="x_grouped", align_bytes=64)
+        x_half = keep.tile([P, HALF, PACK], BF16, name="x_half", align_bytes=64)
+        x_third = keep.tile([P, QUARTER, PACK], BF16, name="x_third", align_bytes=64)
+        x_last = keep.tile([P, QUARTER, PACK], BF16, name="x_last", align_bytes=64)
         x_codes = keep.tile([P, S], U32, name="x_codes", align_bytes=64)
         w_grouped = [keep.tile([P, P, PACK], BF16, name=f"w_grouped{h}", align_bytes=64) for h in range(2)]
         w_codes = keep.tile([P, N], U32, name="w_codes", align_bytes=64)
@@ -59,8 +59,10 @@ def tile_picked_pool_lin_relu_sub_e_kernel(tc, xT, w, b, offs, out):
         x_rows = xT.rearrange("(p j) t -> p j t", j=PACK)
         nc.sync.dma_start(first_pair[:], x_rows[:, 0:2, :])
         nc.sync.dma_start(offsets[:], offs)
-        for i in range(2):
-            nc.vector.memset(zeros[i][:, 0:1], 0.0)
+        early_zero = x_third[:, 0, 3:4]
+        nc.vector.memset(early_zero, 0.0)
+        nc.vector.memset(one[:, 0:1], 1.0)
+        nc.vector.memset(zero[:, 0:1], 0.0)
         nc.sync.dma_start(planes[2][:], x_rows[:, 2, :])
         nc.sync.dma_start(planes[3][:], x_rows[:, 3, :])
         nc.sync.dma_start(w_raw[:], w.rearrange("(p j) m -> p j m", j=PACK))
@@ -108,45 +110,44 @@ def tile_picked_pool_lin_relu_sub_e_kernel(tc, xT, w, b, offs, out):
         def pairs(picked):
             return picked.rearrange("p j n -> p n j")
 
+        last = HALF + QUARTER
         for h, picked in enumerate((picked_half, picked_rest)):
             for t in range(2):
                 nc.vector.tensor_copy(picked[:, t, :], first_pair[:, t, :].indirect(entries(h * HALF, HALF)))
-        nc.scalar.copy(x_grouped[:, :HALF, 0:2], pairs(picked_half[:]))
-        by_vector = BY_VECTOR - HALF
-        nc.vector.tensor_copy(picked_rest[:, 2, :by_vector], planes[2][:].indirect(entries(HALF, by_vector)))
-        nc.vector.tensor_copy(x_grouped[:, :HALF, 2], planes[2][:].indirect(entries(0, HALF)))
-        nc.vector.tensor_copy(x_grouped[:, HALF:BY_VECTOR, 0:3], pairs(picked_rest[:, :, :by_vector]))
-        nc.scalar.activation(picked_rest[:, 2, by_vector:], planes[2][:].indirect(entries(BY_VECTOR, S - BY_VECTOR)), COPY)
-        nc.scalar.copy(x_grouped[:, BY_VECTOR:, 0:3], pairs(picked_rest[:, :, by_vector:]))
-        nc.vector.tensor_copy(x_grouped[:, :BY_VECTOR, 3], planes[3][:].indirect(entries(0, BY_VECTOR)))
-        for picked, a, n in zip(picked_last, starts, SCALAR_PIECES):
-            nc.scalar.activation(picked[:], planes[3][:].indirect(entries(a, n)), COPY)
-        for picked, a, n in zip(picked_last, starts, SCALAR_PIECES):
-            nc.scalar.copy(x_grouped[:, a : a + n, 3], picked[:])
-        nc.scalar.activation(*weight_views(0, 0, W_FIRST), IDENTITY, bias=zeros[0][:, 0:1])
-        nc.scalar.activation(*weight_views(0, W_FIRST, W_SCALAR), IDENTITY, bias=zeros[1][:, 0:1])
+        nc.scalar.copy(x_half[:, :, 0:2], pairs(picked_half[:]))
+        nc.vector.tensor_copy(picked_rest[:, 2, :QUARTER], planes[2][:].indirect(entries(HALF, QUARTER)))
+        nc.vector.tensor_copy(x_half[:, :, 2], planes[2][:].indirect(entries(0, HALF)))
+        nc.vector.tensor_copy(x_third[:, :, 0:3], pairs(picked_rest[:, :, :QUARTER]))
+        nc.scalar.activation(picked_rest[:, 2, QUARTER:], planes[2][:].indirect(entries(last, QUARTER)), COPY)
+        nc.scalar.copy(x_last[:, :, 0:3], pairs(picked_rest[:, :, QUARTER:]))
+
+        nc.vector.tensor_copy(picked_third[:], planes[3][:].indirect(entries(HALF, QUARTER)))
+        nc.vector.tensor_copy(x_half[:, :, 3], planes[3][:].indirect(entries(0, HALF)))
+        for e in range(2):
+            nc.scalar.activation(picked_last[e][:], planes[3][:].indirect(entries(last + e * EIGHTH, EIGHTH)), COPY)
+        for e in range(2):
+            nc.scalar.copy(x_last[:, e * EIGHTH : (e + 1) * EIGHTH, 3], picked_last[e][:])
+
+        nc.scalar.activation(*weight_views(0, 0, W_FIRST), IDENTITY, bias=early_zero, scale=one[:, 0:1])
+        nc.scalar.activation(*weight_views(0, W_FIRST, W_SCALAR), IDENTITY, bias=zero[:, 0:1])
         nc.vector.tensor_copy(*weight_views(0, W_SCALAR, P))
         nc.scalar.copy(*weight_views(1, 0, P))
-        outer_scales = keep.tile([P, HALF], U8, name="outer_scales", tag="zeros_then_scales0", align_bytes=64)
-        middle_scales = keep.tile([P, HALF], U8, name="middle_scales", tag="zeros_then_scales1", align_bytes=64)
-        x_scales = [
-            outer_scales[:, :QUARTER],
-            middle_scales[:, :QUARTER],
-            middle_scales[:, QUARTER:],
-            outer_scales[:, QUARTER:],
-        ]
+        nc.vector.tensor_copy(x_third[:, :, 3], picked_third[:])
+
+        last_scales = keep.tile([P, QUARTER], U8, name="last_scales", tag="one_then_scales", align_bytes=64)
+        other_scales = keep.tile([P, last], U8, name="other_scales", tag="zero_then_scales", align_bytes=64)
+        x_scales = [other_scales[:, q * QUARTER : (q + 1) * QUARTER] for q in range(3)] + [last_scales[:]]
+        x_grouped = [x_half[:, :QUARTER, :], x_half[:, QUARTER:, :], x_third[:], x_last[:]]
 
         def quantize_x(q):
-            cols = slice(q * QUARTER, (q + 1) * QUARTER)
-            quantize(x_codes[:, cols], x_scales[q], x_grouped[:, cols, :])
+            quantize(x_codes[:, q * QUARTER : (q + 1) * QUARTER], x_scales[q], x_grouped[q])
 
         quantize_x(3)
-        quantize_x(0)
         quantize_w(0)
-        quantize_x(1)
-        quantize_x(2)
+        for q in range(3):
+            quantize_x(q)
         quantize_w(1)
-        ready_order = (0, 3, 1, 2)
+        ready_order = (3, 0, 1, 2)
         for q in ready_order:
             product(0, q)
         for q in range(4):

@@ -18,6 +18,7 @@ RELU = mybir.ActivationFunctionType.Relu
 IDENTITY = mybir.ActivationFunctionType.Identity
 ADD = mybir.AluOpType.add
 MAX = mybir.AluOpType.max
+MULT = mybir.AluOpType.mult
 AXIS_X = mybir.AxisListType.X
 
 HALF = S // 2
@@ -42,8 +43,7 @@ def tile_picked_pool_lin_relu_sub_e_kernel(tc, xT, w, b, offs, out):
         picked_third = keep.tile([P, QUARTER], F32, name="picked_third", align_bytes=64)
         picked_last = [keep.tile([P, EIGHTH], F32, name=f"picked_last{e}", align_bytes=64) for e in range(2)]
         w_raw = keep.tile([P, PACK, N], F32, name="w_raw", align_bytes=64)
-        one = keep.tile([P, 64], F32, name="one", tag="one_then_scales", align_bytes=64)
-        zero = keep.tile([P, 96], F32, name="zero", tag="zero_then_scales", align_bytes=64)
+        zeros = [keep.tile([P, 64], F32, name=f"zeros{i}", tag=f"zeros_then_scales{i}", align_bytes=64) for i in range(2)]
         bias = keep.tile([P, 2], F32, name="bias", align_bytes=64)
         x_half = keep.tile([P, HALF, PACK], BF16, name="x_half", align_bytes=64)
         x_third = keep.tile([P, QUARTER, PACK], BF16, name="x_third", align_bytes=64)
@@ -59,10 +59,8 @@ def tile_picked_pool_lin_relu_sub_e_kernel(tc, xT, w, b, offs, out):
         x_rows = xT.rearrange("(p j) t -> p j t", j=PACK)
         nc.sync.dma_start(first_pair[:], x_rows[:, 0:2, :])
         nc.sync.dma_start(offsets[:], offs)
-        early_zero = x_third[:, 0, 3:4]
-        nc.vector.memset(early_zero, 0.0)
-        nc.vector.memset(one[:, 0:1], 1.0)
-        nc.vector.memset(zero[:, 0:1], 0.0)
+        for zero in zeros:
+            nc.vector.memset(zero[:, 0:1], 0.0)
         nc.sync.dma_start(planes[2][:], x_rows[:, 2, :])
         nc.sync.dma_start(planes[3][:], x_rows[:, 3, :])
         nc.sync.dma_start(w_raw[:], w.rearrange("(p j) m -> p j m", j=PACK))
@@ -123,29 +121,37 @@ def tile_picked_pool_lin_relu_sub_e_kernel(tc, xT, w, b, offs, out):
 
         nc.vector.tensor_copy(picked_third[:], planes[3][:].indirect(entries(HALF, QUARTER)))
         nc.vector.tensor_copy(x_half[:, :, 3], planes[3][:].indirect(entries(0, HALF)))
+        nc.gpsimd.tensor_scalar(
+            out=x_third[:, :, 3], in0=picked_third[:], scalar1=1.0, scalar2=0.0, op0=MULT, op1=ADD
+        )
         for e in range(2):
             nc.scalar.activation(picked_last[e][:], planes[3][:].indirect(entries(last + e * EIGHTH, EIGHTH)), COPY)
         for e in range(2):
             nc.scalar.copy(x_last[:, e * EIGHTH : (e + 1) * EIGHTH, 3], picked_last[e][:])
 
-        nc.scalar.activation(*weight_views(0, 0, W_FIRST), IDENTITY, bias=early_zero, scale=one[:, 0:1])
-        nc.scalar.activation(*weight_views(0, W_FIRST, W_SCALAR), IDENTITY, bias=zero[:, 0:1])
+        nc.scalar.activation(*weight_views(0, 0, W_FIRST), IDENTITY, bias=zeros[0][:, 0:1])
+        nc.scalar.activation(*weight_views(0, W_FIRST, W_SCALAR), IDENTITY, bias=zeros[1][:, 0:1])
         nc.vector.tensor_copy(*weight_views(0, W_SCALAR, P))
         nc.scalar.copy(*weight_views(1, 0, P))
-        nc.vector.tensor_copy(x_third[:, :, 3], picked_third[:])
 
-        last_scales = keep.tile([P, QUARTER], U8, name="last_scales", tag="one_then_scales", align_bytes=64)
-        other_scales = keep.tile([P, last], U8, name="other_scales", tag="zero_then_scales", align_bytes=64)
-        x_scales = [other_scales[:, q * QUARTER : (q + 1) * QUARTER] for q in range(3)] + [last_scales[:]]
+        outer_scales = keep.tile([P, HALF], U8, name="outer_scales", tag="zeros_then_scales0", align_bytes=64)
+        middle_scales = keep.tile([P, HALF], U8, name="middle_scales", tag="zeros_then_scales1", align_bytes=64)
+        x_scales = [
+            outer_scales[:, :QUARTER],
+            middle_scales[:, :QUARTER],
+            middle_scales[:, QUARTER:],
+            outer_scales[:, QUARTER:],
+        ]
         x_grouped = [x_half[:, :QUARTER, :], x_half[:, QUARTER:, :], x_third[:], x_last[:]]
 
         def quantize_x(q):
             quantize(x_codes[:, q * QUARTER : (q + 1) * QUARTER], x_scales[q], x_grouped[q])
 
         quantize_x(3)
+        quantize_x(0)
         quantize_w(0)
-        for q in range(3):
-            quantize_x(q)
+        quantize_x(1)
+        quantize_x(2)
         quantize_w(1)
         ready_order = (3, 0, 1, 2)
         for q in ready_order:

@@ -26,7 +26,7 @@ QUARTER = S // 4
 EIGHTH = S // 8
 LIST_COLS = S // 16
 W_FIRST = 4
-W_SCALAR = 64
+W_SCALAR = 56
 
 
 def tile_picked_pool_lin_relu_sub_e_kernel(tc, xT, w, b, offs, out):
@@ -43,7 +43,7 @@ def tile_picked_pool_lin_relu_sub_e_kernel(tc, xT, w, b, offs, out):
         picked_third = keep.tile([P, QUARTER], F32, name="picked_third", align_bytes=64)
         picked_last = [keep.tile([P, EIGHTH], F32, name=f"picked_last{e}", align_bytes=64) for e in range(2)]
         w_raw = keep.tile([P, PACK, N], F32, name="w_raw", align_bytes=64)
-        zeros = [keep.tile([P, 64], F32, name=f"zeros{i}", tag=f"zeros_then_scales{i}", align_bytes=64) for i in range(2)]
+        zeros = [keep.tile([P, 96], F32, name=f"zeros{i}", tag=f"zeros_then_scales{i}", align_bytes=64) for i in range(2)]
         bias = keep.tile([P, 2], F32, name="bias", align_bytes=64)
         x_half = keep.tile([P, HALF, PACK], BF16, name="x_half", align_bytes=64)
         x_third = keep.tile([P, QUARTER, PACK], BF16, name="x_third", align_bytes=64)
@@ -134,22 +134,17 @@ def tile_picked_pool_lin_relu_sub_e_kernel(tc, xT, w, b, offs, out):
         nc.vector.tensor_copy(*weight_views(0, W_SCALAR, P))
         nc.scalar.copy(*weight_views(1, 0, P))
 
-        outer_scales = keep.tile([P, HALF], U8, name="outer_scales", tag="zeros_then_scales0", align_bytes=64)
-        middle_scales = keep.tile([P, HALF], U8, name="middle_scales", tag="zeros_then_scales1", align_bytes=64)
-        x_scales = [
-            outer_scales[:, :QUARTER],
-            middle_scales[:, :QUARTER],
-            middle_scales[:, QUARTER:],
-            outer_scales[:, QUARTER:],
-        ]
+        last_scales = keep.tile([P, QUARTER], U8, name="last_scales", tag="zeros_then_scales0", align_bytes=64)
+        other_scales = keep.tile([P, last], U8, name="other_scales", tag="zeros_then_scales1", align_bytes=64)
+        x_scales = [other_scales[:, q * QUARTER : (q + 1) * QUARTER] for q in range(3)] + [last_scales[:]]
         x_grouped = [x_half[:, :QUARTER, :], x_half[:, QUARTER:, :], x_third[:], x_last[:]]
 
         def quantize_x(q):
             quantize(x_codes[:, q * QUARTER : (q + 1) * QUARTER], x_scales[q], x_grouped[q])
 
         quantize_x(3)
-        quantize_x(0)
         quantize_w(0)
+        quantize_x(0)
         quantize_x(1)
         quantize_x(2)
         quantize_w(1)

@@ -23,10 +23,11 @@ AXIS_X = mybir.AxisListType.X
 
 HALF = S // 2
 QUARTER = S // 4
-EIGHTH = S // 8
+SCALAR_PIECES = (96, 64)
+PLAIN = HALF - sum(SCALAR_PIECES)
 LIST_COLS = S // 16
 W_FIRST = 4
-W_SCALAR = 56
+W_SCALAR = (24, 32)
 
 
 def tile_picked_pool_lin_relu_sub_e_kernel(tc, xT, w, b, offs, out):
@@ -40,14 +41,13 @@ def tile_picked_pool_lin_relu_sub_e_kernel(tc, xT, w, b, offs, out):
         planes = {t: keep.tile([P, T], F32, name=f"plane{t}", align_bytes=64) for t in (2, 3)}
         picked_half = keep.tile([P, 2, HALF], F32, name="picked_half", align_bytes=64)
         picked_rest = keep.tile([P, 3, HALF], F32, name="picked_rest", align_bytes=64)
-        picked_third = keep.tile([P, QUARTER], F32, name="picked_third", align_bytes=64)
-        picked_last = [keep.tile([P, EIGHTH], F32, name=f"picked_last{e}", align_bytes=64) for e in range(2)]
+        picked_plain = keep.tile([P, PLAIN], BF16, name="picked_plain", align_bytes=64)
+        picked_last = [keep.tile([P, n], F32, name=f"picked_last{n}", align_bytes=64) for n in SCALAR_PIECES]
         w_raw = keep.tile([P, PACK, N], F32, name="w_raw", align_bytes=64)
         zeros = [keep.tile([P, 96], F32, name=f"zeros{i}", tag=f"zeros_then_scales{i}", align_bytes=64) for i in range(2)]
         bias = keep.tile([P, 2], F32, name="bias", align_bytes=64)
         x_half = keep.tile([P, HALF, PACK], BF16, name="x_half", align_bytes=64)
-        x_third = keep.tile([P, QUARTER, PACK], BF16, name="x_third", align_bytes=64)
-        x_last = keep.tile([P, QUARTER, PACK], BF16, name="x_last", align_bytes=64)
+        x_rest = keep.tile([P, HALF, PACK], BF16, name="x_rest", align_bytes=64)
         x_codes = keep.tile([P, S], U32, name="x_codes", align_bytes=64)
         w_grouped = [keep.tile([P, P, PACK], BF16, name=f"w_grouped{h}", align_bytes=64) for h in range(2)]
         w_codes = keep.tile([P, N], U32, name="w_codes", align_bytes=64)
@@ -77,8 +77,9 @@ def tile_picked_pool_lin_relu_sub_e_kernel(tc, xT, w, b, offs, out):
         def quantize(codes, scales, grouped):
             nc.vector.quantize_mx(out=codes.bitcast(FP8X4), scales=scales, in_=grouped.rearrange("p n j -> p (n j)"))
 
-        def quantize_w(m):
-            quantize(w_codes[:, m * P : (m + 1) * P], w_scales[:, m * P : (m + 1) * P], w_grouped[m][:])
+        def quantize_w(m, a, z):
+            cols = slice(m * P + a, m * P + z)
+            quantize(w_codes[:, cols], w_scales[:, cols], w_grouped[m][:, a:z, :])
 
         def product(m, q):
             nc.tensor.matmul_mx(
@@ -115,39 +116,45 @@ def tile_picked_pool_lin_relu_sub_e_kernel(tc, xT, w, b, offs, out):
         nc.scalar.copy(x_half[:, :, 0:2], pairs(picked_half[:]))
         nc.vector.tensor_copy(picked_rest[:, 2, :QUARTER], planes[2][:].indirect(entries(HALF, QUARTER)))
         nc.vector.tensor_copy(x_half[:, :, 2], planes[2][:].indirect(entries(0, HALF)))
-        nc.vector.tensor_copy(x_third[:, :, 0:3], pairs(picked_rest[:, :, :QUARTER]))
+        nc.vector.tensor_copy(x_rest[:, :PLAIN, 0:3], pairs(picked_rest[:, :, :PLAIN]))
         nc.scalar.activation(picked_rest[:, 2, QUARTER:], planes[2][:].indirect(entries(last, QUARTER)), COPY)
-        nc.scalar.copy(x_last[:, :, 0:3], pairs(picked_rest[:, :, QUARTER:]))
+        nc.scalar.copy(x_rest[:, PLAIN:, 0:3], pairs(picked_rest[:, :, PLAIN:]))
 
-        nc.vector.tensor_copy(picked_third[:], planes[3][:].indirect(entries(HALF, QUARTER)))
+        nc.vector.tensor_copy(picked_plain[:], planes[3][:].indirect(entries(HALF, PLAIN)))
         nc.vector.tensor_copy(x_half[:, :, 3], planes[3][:].indirect(entries(0, HALF)))
         nc.gpsimd.tensor_scalar(
-            out=x_third[:, :, 3], in0=picked_third[:], scalar1=1.0, scalar2=0.0, op0=MULT, op1=ADD
+            out=x_rest[:, :PLAIN, 3], in0=picked_plain[:], scalar1=1.0, scalar2=0.0, op0=MULT, op1=ADD
         )
-        for e in range(2):
-            nc.scalar.activation(picked_last[e][:], planes[3][:].indirect(entries(last + e * EIGHTH, EIGHTH)), COPY)
-        for e in range(2):
-            nc.scalar.copy(x_last[:, e * EIGHTH : (e + 1) * EIGHTH, 3], picked_last[e][:])
+        starts = (HALF - SCALAR_PIECES[0], PLAIN)
+        for picked, a, n in zip(picked_last, starts, SCALAR_PIECES):
+            nc.scalar.activation(picked[:], planes[3][:].indirect(entries(HALF + a, n)), COPY)
+        for picked, a, n in zip(picked_last, starts, SCALAR_PIECES):
+            nc.scalar.copy(x_rest[:, a : a + n, 3], picked[:])
 
         nc.scalar.activation(*weight_views(0, 0, W_FIRST), IDENTITY, bias=zeros[0][:, 0:1])
-        nc.scalar.activation(*weight_views(0, W_FIRST, W_SCALAR), IDENTITY, bias=zeros[1][:, 0:1])
-        nc.vector.tensor_copy(*weight_views(0, W_SCALAR, P))
-        nc.scalar.copy(*weight_views(1, 0, P))
+        nc.scalar.copy(*weight_views(0, W_FIRST, W_SCALAR[0]))
+        nc.scalar.activation(*weight_views(0, P // 2, P // 2 + W_SCALAR[1]), IDENTITY, bias=zeros[1][:, 0:1])
+        nc.vector.tensor_copy(*weight_views(0, W_SCALAR[0], P // 2))
+        nc.vector.tensor_copy(*weight_views(0, P // 2 + W_SCALAR[1], P))
+        nc.scalar.copy(*weight_views(1, 0, P // 2))
+        nc.scalar.copy(*weight_views(1, P // 2, P))
 
         last_scales = keep.tile([P, QUARTER], U8, name="last_scales", tag="zeros_then_scales0", align_bytes=64)
         other_scales = keep.tile([P, last], U8, name="other_scales", tag="zeros_then_scales1", align_bytes=64)
         x_scales = [other_scales[:, q * QUARTER : (q + 1) * QUARTER] for q in range(3)] + [last_scales[:]]
-        x_grouped = [x_half[:, :QUARTER, :], x_half[:, QUARTER:, :], x_third[:], x_last[:]]
+        x_grouped = [x_half[:, :QUARTER, :], x_half[:, QUARTER:, :], x_rest[:, :QUARTER, :], x_rest[:, QUARTER:, :]]
 
         def quantize_x(q):
             quantize(x_codes[:, q * QUARTER : (q + 1) * QUARTER], x_scales[q], x_grouped[q])
 
         quantize_x(3)
-        quantize_w(0)
+        quantize_w(0, 0, P // 2)
+        quantize_w(0, P // 2, P)
         quantize_x(0)
         quantize_x(1)
         quantize_x(2)
-        quantize_w(1)
+        quantize_w(1, 0, P // 2)
+        quantize_w(1, P // 2, P)
         ready_order = (3, 0, 1, 2)
         for q in ready_order:
             product(0, q)

from contextlib import ExitStack

import concourse.mybir as mybir

K, T, D, S, V, N = 512, 2048, 4, 512, 128, 256
P = 128
PACK = 4
FLOPS = 2 * K * S * N

F32 = mybir.dt.float32
BF16 = mybir.dt.bfloat16
U32 = mybir.dt.uint32
U16 = mybir.dt.uint16
U8 = mybir.dt.uint8
FP8X4 = mybir.dt.float8_e4m3fn_x4
COPY = mybir.ActivationFunctionType.Copy
RELU = mybir.ActivationFunctionType.Relu
IDENTITY = mybir.ActivationFunctionType.Identity
ADD = mybir.AluOpType.add
MAX = mybir.AluOpType.max
MULT = mybir.AluOpType.mult
AXIS_X = mybir.AxisListType.X

HALF = S // 2
QUARTER = S // 4
SCALAR_PIECES = (96, 64)
PLAIN = HALF - sum(SCALAR_PIECES)
LIST_COLS = S // 16
W_FIRST = 4
W_SCALAR = (24, 32)


def tile_picked_pool_lin_relu_sub_e_kernel(tc, xT, w, b, offs, out):
    nc = tc.nc
    with ExitStack() as ctx:
        keep = ctx.enter_context(tc.tile_pool(name="keep", bufs=1))
        psum = ctx.enter_context(tc.psum_pool(name="psum", bufs=1))

        offsets = keep.tile([P, LIST_COLS], U16, name="offsets")
        first_pair = keep.tile([P, 2, T], F32, name="first_pair", align_bytes=64)
        planes = {t: keep.tile([P, T], F32, name=f"plane{t}", align_bytes=64) for t in (2, 3)}
        picked_half = keep.tile([P, 2, HALF], F32, name="picked_half", align_bytes=64)
        picked_rest = keep.tile([P, 3, HALF], F32, name="picked_rest", align_bytes=64)
        picked_plain = keep.tile([P, PLAIN], BF16, name="picked_plain", align_bytes=64)
        picked_last = [keep.tile([P, n], F32, name=f"picked_last{n}", align_bytes=64) for n in SCALAR_PIECES]
        w_raw = keep.tile([P, PACK, N], F32, name="w_raw", align_bytes=64)
        zeros = [keep.tile([P, 96], F32, name=f"zeros{i}", tag=f"zeros_then_scales{i}", align_bytes=64) for i in range(2)]
        bias = keep.tile([P, 2], F32, name="bias", align_bytes=64)
        x_half = keep.tile([P, HALF, PACK], BF16, name="x_half", align_bytes=64)
        x_rest = keep.tile([P, HALF, PACK], BF16, name="x_rest", align_bytes=64)
        x_codes = keep.tile([P, S], U32, name="x_codes", align_bytes=64)
        w_grouped = [keep.tile([P, P, PACK], BF16, name=f"w_grouped{h}", align_bytes=64) for h in range(2)]
        w_codes = keep.tile([P, N], U32, name="w_codes", align_bytes=64)
        w_scales = keep.tile([P, N], U8, name="w_scales", align_bytes=64)
        accs = {(m, q): psum.tile([P, QUARTER], F32, name=f"acc{m}_{q}") for m in range(2) for q in range(4)}
        pooled = [keep.tile([P, V], F32, name=f"pooled{m}") for m in range(2)]
        results = keep.tile([P, 2, V], F32, name="results")

        x_rows = xT.rearrange("(p j) t -> p j t", j=PACK)
        nc.sync.dma_start(first_pair[:], x_rows[:, 0:2, :])
        nc.sync.dma_start(offsets[:], offs)
        for zero in zeros:
            nc.vector.memset(zero[:, 0:1], 0.0)
        nc.sync.dma_start(planes[2][:], x_rows[:, 2, :])
        nc.sync.dma_start(planes[3][:], x_rows[:, 3, :])
        nc.sync.dma_start(w_raw[:], w.rearrange("(p j) m -> p j m", j=PACK))
        nc.sync.dma_start(bias[:], b.rearrange("(p h) o -> p (h o)", h=2))

        def entries(a, n):
            return offsets[:, a // 16 : (a + n) // 16]

        def weight_views(m, a, z):
            dst = w_grouped[m][:, a:z, :].rearrange("p (c i) j -> p c j i", i=4)
            src = w_raw[:, :, 2 * a : 2 * z].rearrange("p j (c i h) -> p h c j i", i=4, h=2)[:, m]
            return dst, src

        def quantize(codes, scales, grouped):
            nc.vector.quantize_mx(out=codes.bitcast(FP8X4), scales=scales, in_=grouped.rearrange("p n j -> p (n j)"))

        def quantize_w(m, a, z):
            cols = slice(m * P + a, m * P + z)
            quantize(w_codes[:, cols], w_scales[:, cols], w_grouped[m][:, a:z, :])

        def product(m, q):
            nc.tensor.matmul_mx(
                out=accs[m, q][:],
                lhsT=w_codes[:, m * P : (m + 1) * P].bitcast(FP8X4),
                lhsT_scale=w_scales[:, m * P : (m + 1) * P],
                rhs=x_codes[:, q * QUARTER : (q + 1) * QUARTER].bitcast(FP8X4),
                rhs_scale=x_scales[q],
                start=True,
                stop=True,
            )

        def largest(m, q):
            nc.vector.tensor_reduce(
                out=pooled[m][:, q * QUARTER // D : (q + 1) * QUARTER // D],
                in_=accs[m, q][:].rearrange("p (v d) -> p v d", d=D),
                axis=AXIS_X,
                op=MAX,
            )

        def store(a, z):
            nc.sync.dma_start(
                out.rearrange("(p m) v -> p (m v)", m=2)[:, a:z],
                results[:].rearrange("p m v -> p (m v)")[:, a:z],
            )

        def pairs(picked):
            return picked.rearrange("p j n -> p n j")

        last = HALF + QUARTER
        for h, picked in enumerate((picked_half, picked_rest)):
            for t in range(2):
                nc.vector.tensor_copy(picked[:, t, :], first_pair[:, t, :].indirect(entries(h * HALF, HALF)))
        nc.scalar.copy(x_half[:, :, 0:2], pairs(picked_half[:]))
        nc.vector.tensor_copy(picked_rest[:, 2, :QUARTER], planes[2][:].indirect(entries(HALF, QUARTER)))
        nc.vector.tensor_copy(x_half[:, :, 2], planes[2][:].indirect(entries(0, HALF)))
        nc.vector.tensor_copy(x_rest[:, :PLAIN, 0:3], pairs(picked_rest[:, :, :PLAIN]))
        nc.scalar.activation(picked_rest[:, 2, QUARTER:], planes[2][:].indirect(entries(last, QUARTER)), COPY)
        nc.scalar.copy(x_rest[:, PLAIN:, 0:3], pairs(picked_rest[:, :, PLAIN:]))

        nc.vector.tensor_copy(picked_plain[:], planes[3][:].indirect(entries(HALF, PLAIN)))
        nc.vector.tensor_copy(x_half[:, :, 3], planes[3][:].indirect(entries(0, HALF)))
        nc.gpsimd.tensor_scalar(
            out=x_rest[:, :PLAIN, 3], in0=picked_plain[:], scalar1=1.0, scalar2=0.0, op0=MULT, op1=ADD
        )
        starts = (HALF - SCALAR_PIECES[0], PLAIN)
        for picked, a, n in zip(picked_last, starts, SCALAR_PIECES):
            nc.scalar.activation(picked[:], planes[3][:].indirect(entries(HALF + a, n)), COPY)
        for picked, a, n in zip(picked_last, starts, SCALAR_PIECES):
            nc.scalar.copy(x_rest[:, a : a + n, 3], picked[:])

        nc.scalar.activation(*weight_views(0, 0, W_FIRST), IDENTITY, bias=zeros[0][:, 0:1])
        nc.scalar.copy(*weight_views(0, W_FIRST, W_SCALAR[0]))
        nc.scalar.activation(*weight_views(0, P // 2, P // 2 + W_SCALAR[1]), IDENTITY, bias=zeros[1][:, 0:1])
        nc.vector.tensor_copy(*weight_views(0, W_SCALAR[0], P // 2))
        nc.vector.tensor_copy(*weight_views(0, P // 2 + W_SCALAR[1], P))
        nc.scalar.copy(*weight_views(1, 0, P // 2))
        nc.scalar.copy(*weight_views(1, P // 2, P))

        last_scales = keep.tile([P, QUARTER], U8, name="last_scales", tag="zeros_then_scales0", align_bytes=64)
        other_scales = keep.tile([P, last], U8, name="other_scales", tag="zeros_then_scales1", align_bytes=64)
        x_scales = [other_scales[:, q * QUARTER : (q + 1) * QUARTER] for q in range(3)] + [last_scales[:]]
        x_grouped = [x_half[:, :QUARTER, :], x_half[:, QUARTER:, :], x_rest[:, :QUARTER, :], x_rest[:, QUARTER:, :]]

        def quantize_x(q):
            quantize(x_codes[:, q * QUARTER : (q + 1) * QUARTER], x_scales[q], x_grouped[q])

        quantize_x(3)
        quantize_w(0, 0, P // 2)
        quantize_w(0, P // 2, P)
        quantize_x(0)
        quantize_x(1)
        quantize_x(2)
        quantize_w(1, 0, P // 2)
        quantize_w(1, P // 2, P)
        ready_order = (3, 0, 1, 2)
        for q in ready_order:
            product(0, q)
        for q in range(4):
            product(1, q)
        for q in ready_order:
            largest(0, q)
        nc.scalar.activation(results[:, 0, :], pooled[0][:], RELU, bias=bias[:, 0:1])
        largest(1, 0)
        nc.scalar.activation(results[:, 1, : V // 4], pooled[1][:, : V // 4], RELU, bias=bias[:, 1:2])
        store(0, 5 * V // 4)
        for q in range(1, 4):
            largest(1, q)
        nc.vector.tensor_scalar(
            out=results[:, 1, V // 4 :], in0=pooled[1][:, V // 4 :], scalar1=bias[:, 1:2], scalar2=0.0, op0=ADD, op1=MAX
        )
        store(5 * V // 4, 2 * V)
